import numpy as np
CORES = [16,17,18,19,150,151]
N = 6
W = 1024
def setup_inputs(rng):
    amp = 0.5 + 1.5 * rng.random((2, N, 128, 1), dtype=np.float32)
    return {"u": amp[0] * rng.standard_normal((N, 128, W), dtype=np.float32), "b": amp[1] * rng.standard_normal((N, 128, W), dtype=np.float32)}
def setup_inputs_big(rng):
    d = setup_inputs(rng)
    for k in ("u", "b"): d[k] = (d[k].astype(np.float32) * 1024.0).astype(d[k].dtype)
    return d
def setup_inputs_small(rng):
    d = setup_inputs(rng)
    for k in ("u", "b"): d[k] = (d[k].astype(np.float32) * (1 / 1024.0)).astype(d[k].dtype)
    return d
def setup_inputs_apart(rng):
    d = setup_inputs(rng)
    f = (10.0 ** rng.permutation(np.linspace(-1.5, 1.5, N))).astype(np.float32).reshape(N, 1, 1)
    for k in ("u", "b"): d[k] = (d[k].astype(np.float32) * f).astype(d[k].dtype)
    return d
def reference(u, b):
    g = np.concatenate(list(u.astype(np.float64)), axis=1); bb = np.concatenate(list(b.astype(np.float64)), axis=1)
    p = np.concatenate([g[:, -2:], g, g[:, :2]], axis=1)
    n = 0.125 * (p[:, :-4] + p[:, 1:-3] + p[:, 3:-1] + p[:, 4:]) + 0.5 * bb
    d = n - g
    s = np.stack([(d ** 2).mean(axis=1), np.abs(d).max(axis=1)], axis=1)
    return {"y": np.stack([n[:, W * r:W * r + W] for r in range(N)]).astype(np.float32), "s": np.broadcast_to(s.astype(np.float32), (N, 128, 2))}

@@ -1,0 +1,280 @@
+from concourse.bass import DstId, RemoteDMATransfer
+from concourse.mybir import AluOpType
+
+N = 6
+W = 1024
+CW = 256
+ORDER = [1, 2, 0, 3]
+PIECE = {1: (CW - 2, 2 * CW + 2), 2: (2 * CW + 2, 3 * CW + 2), 0: (0, CW - 2), 3: (3 * CW + 2, W)}
+
+SCRATCH = {
+    "U": ("sbuf", [128, W + 4], "float32"),
+    "B": ("sbuf", [128, W], "float32"),
+    "EB": ("sbuf", [128, 4], "float32"),
+    "Q": ("sbuf", [128, W], "float32"),
+    "E": ("sbuf", [128, W], "float32"),
+    "SQ": ("sbuf", [128, W], "float32"),
+    "Y": ("sbuf", [128, W], "float32"),
+    "Z": ("sbuf", [128, 1057], "float32"),
+    "I4": ("sbuf", [128, 128], "float32"),
+    "I8": ("sbuf", [128, 128], "float32"),
+    "ONES": ("sbuf", [128, 1], "float32"),
+    "KS": ("sbuf", [128, 1], "float32"),
+    "MA": ("sbuf", [128, 128], "float32"),
+    "MI": ("sbuf", [128, 128], "float32"),
+    "STS": ("sbuf", [128, 128], "float32"),
+    "TA": ("sbuf", [128, 64], "float32"),
+    "TR": ("sbuf", [128, 128], "float32"),
+    "G": ("sbuf", [128, 4 * N], "float32"),
+    "T1": ("sbuf", [128, 8], "float32"),
+    "T2": ("sbuf", [128, 2], "float32"),
+    "SO": ("sbuf", [128, 2], "float32"),
+    "R0": ("psum", [128, 512], "float32"),
+    "R1": ("psum", [128, 512], "float32"),
+    "R2": ("psum", [128, 512], "float32"),
+    "R3": ("psum", [128, 512], "float32"),
+    "TC": ("psum", [128, 512], "float32"),
+    "ST": ("psum", [128, 512], "float32"),
+    "ZP": ("psum", [128, 512], "float32"),
+}
+SEMAPHORES = ["vs", "se", "su0", "su1", "su2", "su3", "sb0", "sb1", "sb2", "sb3", "sfr", "tr0", "tr1", "tr2", "tr3",
+              "tst", "tfin", "hal", "gs", "loc", "sy1", "sy2", "ss"]
+
+
+def _bits(m):
+    return [i for i in range(m.bit_length()) if (m >> i) & 1]
+
+
+def _mk(bits):
+    m = 0
+    for i in bits:
+        m |= 1 << i
+    return m
+
+
+def _low(topo, cores, c):
+    low = -1
+    for d in cores:
+        if d != c:
+            low &= topo.mask(c, d)
+    return low
+
+
+def _halo_masks(topo, cores, c, dl, dr):
+    low = _low(topo, cores, c)
+    hl, hr = topo.mask(c, dl) & ~low, topo.mask(c, dr) & ~low
+    if hr:
+        return low, hr
+    if hl:
+        return hl, low
+    b = _bits(low)
+    return _mk(b[:len(b) // 2]), _mk(b[len(b) // 2:])
+
+
+def _stat_mask(topo, cores, c, d):
+    low = _low(topo, cores, c)
+    hi = topo.mask(c, d) & ~low
+    return hi if hi else low
+
+
+def rank_program(g, core, T, topo):
+    r = T.rank_of(core)
+    if r is None:
+        return
+    cores = list(T.cores)
+    v, te, sq_, sc = g.vector, g.tensor, g.sync, g.scalar
+    S = T.sem
+    ADD, SUB, MUL, MAX, MIN = AluOpType.add, AluOpType.subtract, AluOpType.mult, AluOpType.max, AluOpType.min
+    R = [T.R0, T.R1, T.R2, T.R3]
+    su = [S.su0, S.su1, S.su2, S.su3]
+    sb = [S.sb0, S.sb1, S.sb2, S.sb3]
+    tr = [S.tr0, S.tr1, S.tr2, S.tr3]
+    left, right = cores[(r - 1) % N], cores[(r + 1) % N]
+
+    n = [0]
+
+    def vw():
+        if n[0]:
+            v.wait_ge(S.vs, n[0])
+
+    def tt(out, a, b, op):
+        vw()
+        v.tensor_tensor(out, a, b, op).then_inc(S.vs, 1)
+        n[0] += 1
+        return n[0]
+
+    def ms(ap, c):
+        vw()
+        v.memset(ap, c).then_inc(S.vs, 1)
+        n[0] += 1
+        return n[0]
+
+    def Us(c, s):
+        return T.U[:, c * CW + 2 + s:c * CW + 2 + s + CW]
+
+    def blk(t, c):
+        return t[:, c * CW:(c + 1) * CW]
+
+    ms(T.Z[0:1, :], 0.0)
+    ms(T.Z[0:1, 0:1057:33], 4.0)
+    z_done = ms(T.I4[:], 0.0)
+    ms(T.ZP[:, 320:448], -2.0)
+    C = T.TC[:, 256:512]
+    ms(C, 0.125)
+    ms(T.ZP[:, 0:128], 0.0)
+    ms(T.MA[:], 0.0)
+    ms(T.MI[:], 0.0)
+    ms(T.ONES[:], 1.0)
+    ms(T.KS[:], 1.0 / (32.0 * N * W))
+    t = T.TC[:, 0:CW]
+    i8_done = 0
+    for c in (1, 2):
+        v.wait_ge(su[c], 16)
+        tt(t, Us(c, -2), Us(c, -1), ADD)
+        tt(t, t, Us(c, 1), ADD)
+        tt(blk(T.Q, c), t, Us(c, 2), ADD)
+        if c == 1:
+            v.wait_ge(S.sfr, 64)
+            i8_done = tt(T.I8[:], T.I4[:], T.ZP[:, 320:448], MUL)
+
+    sq_done = {}
+    hal_n = (len(_bits(_halo_masks(topo, cores, left, cores[(r - 2) % N], core)[1]))
+             + len(_bits(_halo_masks(topo, cores, right, core, cores[(r + 2) % N])[0])))
+
+    def phase2(c, shifts=None):
+        Rc = R[c][:, 0:CW]
+        v.wait_ge(tr[c], 1)
+        if shifts is None:
+            tt(blk(T.E, c), blk(T.Q, c), Rc, ADD)
+        else:
+            v.wait_ge(su[c], 16)
+            tt(Rc, Rc, Us(c, shifts[0]), ADD)
+            tt(Rc, Rc, Us(c, shifts[1]), ADD)
+            v.wait_ge(S.hal, hal_n)
+            tt(Rc, Rc, Us(c, shifts[2]), ADD)
+            tt(blk(T.E, c), Rc, Us(c, shifts[3]), ADD)
+        tt(Rc, blk(T.E, c), C, MUL)
+        sq_done[c] = tt(blk(T.SQ, c), Rc, blk(T.E, c), MUL)
+        for h in (0, 1):
+            tt(T.MA[:], T.MA[:], R[c][:, 128 * h:128 * h + 128], MAX)
+            tt(T.MI[:], T.MI[:], R[c][:, 128 * h:128 * h + 128], MIN)
+
+    phase2(1)
+    phase2(2)
+    phase2(0, (1, 2, -1, -2))
+    phase2(3, (-1, -2, 1, 2))
+    tt(T.ZP[:, 128:256], T.ZP[:, 0:128], T.MI[:], SUB)
+    tt(T.ZP[:, 256:320], T.MA[:, 0:64], T.ZP[:, 128:192], MAX)
+    tt(T.TA[:], T.MA[:, 64:128], T.ZP[:, 192:256], MAX)
+    v.wait_ge(S.tst, 1)
+    vw()
+    v.tensor_copy(T.STS[:], T.ST[:, 0:128]).then_inc(S.vs, 1)
+    n[0] += 1
+    sts_done = n[0]
+    tt(T.TR[:, 0:64], T.ZP[:, 256:320], T.TA[:], MAX)
+    o, w = 0, 32
+    while w >= 2:
+        tt(T.TR[:, o + 2 * w:o + 3 * w], T.TR[:, o:o + w], T.TR[:, o + w:o + 2 * w], MAX)
+        o, w = o + 2 * w, w // 2
+    own = T.G[:, 4 * r:4 * r + 2]
+    tt(T.G[:, 4 * r + 1:4 * r + 2], T.TR[:, o:o + 1], T.TR[:, o + 1:o + 2], MAX)
+    v.wait_ge(S.tfin, 1)
+    part_done = tt(T.G[:, 4 * r:4 * r + 1], T.ST[:, 128:129], T.KS[:], MUL)
+    y_done = {}
+    for c in ORDER:
+        y_done[c] = tt(blk(T.Y, c), R[c][:, 0:CW], Us(c, 0), ADD)
+    g_n = 0
+    for d in cores:
+        if d != core:
+            g_n += len(_bits(_stat_mask(topo, cores, d, core)))
+    v.wait_ge(S.gs, g_n)
+    tt(T.T1[:, 0:3], T.G[:, 0:12:4], T.G[:, 12:24:4], ADD)
+    tt(T.T1[:, 4:7], T.G[:, 1:12:4], T.G[:, 13:24:4], MAX)
+    tt(T.T2[:, 0:1], T.T1[:, 0:1], T.T1[:, 1:2], ADD)
+    tt(T.T2[:, 1:2], T.T1[:, 4:5], T.T1[:, 5:6], MAX)
+    tt(T.SO[:, 0:1], T.T2[:, 0:1], T.T1[:, 2:3], ADD)
+    all_done = tt(T.SO[:, 1:2], T.T2[:, 1:2], T.T1[:, 6:7], MAX)
+
+    te.wait_ge(S.sfr, 64)
+
+    def seed(c):
+        te.wait_ge(sb[c], 16)
+        te.wait_ge(su[c], 16)
+        te.matmul(R[c][:, 0:CW], T.I4[:], blk(T.B, c), True, False)
+        te.wait_ge(S.vs, i8_done)
+        te.matmul(R[c][:, 0:CW], T.I8[:], Us(c, 0), False, True).then_inc(tr[c], 1)
+
+    def sums(c, first, last):
+        te.wait_ge(S.vs, sq_done[c])
+        for h in (0, 1):
+            m = te.matmul(T.ST[:, 0:128], T.SQ[:, c * CW + 128 * h:c * CW + 128 * h + 128], T.I4[:],
+                          first and h == 0, last and h == 1)
+            if last and h == 1:
+                m.then_inc(S.tst, 1)
+
+    seed(1)
+    seed(2)
+    seed(0)
+    sums(1, True, False)
+    seed(3)
+    sums(2, False, False)
+    sums(0, False, False)
+    sums(3, False, True)
+    te.wait_ge(S.vs, sts_done)
+    te.matmul(T.ST[:, 128:129], T.STS[:], T.ONES[:], True, True).then_inc(S.tfin, 1)
+
+    def load_u(q, c):
+        a, b = PIECE[c]
+        q.dma_start(T.U[:, a + 2:b + 2], T.u[:, a:b]).then_inc(su[c], 16)
+
+    def load_b(q, c):
+        q.dma_start(blk(T.B, c), blk(T.b, c)).then_inc(sb[c], 16)
+
+    sq_.dma_start(T.EB[:, 0:2], T.u[:, 0:2]).then_inc(S.se, 16)
+    sq_.dma_start(T.EB[:, 2:4], T.u[:, W - 2:W]).then_inc(S.se, 16)
+    load_u(sq_, 1)
+    load_b(sq_, 1)
+    load_u(sq_, 2)
+    load_u(sq_, 0)
+    load_u(sq_, 3)
+    sc.wait_ge(S.vs, z_done)
+    sc.dma_start(T.I4[0:33, 0:32], T.Z[0:1, 0:1056]).then_inc(S.sfr, 16)
+    for k in (1, 2, 3):
+        sc.dma_start(T.I4[32 * k - 1:32 * k + 32, 32 * k:32 * k + 32], T.Z[0:1, 1:1057]).then_inc(S.sfr, 16)
+    load_b(sc, 2)
+    load_b(sc, 0)
+    load_b(sc, 3)
+    for k, c in enumerate(ORDER):
+        q, sem = ((sq_, S.sy1), (sc, S.sy2))[k % 2]
+        q.wait_ge(S.vs, y_done[c])
+        q.dma_start(blk(T.y, c), blk(T.Y, c)).then_inc(sem, 16)
+    sq_.wait_ge(S.vs, all_done)
+    sq_.dma_start(T.s[:], T.SO[:]).then_inc(S.ss, 16)
+    sq_.wait_ge(S.sy1, 32)
+    sq_.wait_ge(S.ss, 16)
+    sc.wait_ge(S.sy2, 32)
+
+    def dst(d):
+        rid, pid = topo.addr(d, core)
+        return DstId(rid=rid, pnc=pid)
+
+    ml, mr = _halo_masks(topo, cores, core, left, right)
+    g.wait_ge(S.se, 32)
+    g.remote_dma_fused([
+        RemoteDMATransfer(dst_ids=[dst(left)], dma_engine_mask=ml, remote_sem=S.hal, src=T.EB[:, 0:2], dst=T.U[:, W + 2:W + 4]),
+        RemoteDMATransfer(dst_ids=[dst(right)], dma_engine_mask=mr, remote_sem=S.hal, src=T.EB[:, 2:4], dst=T.U[:, 0:2]),
+    ], local_sem=S.loc)
+    loc_n = len(_bits(ml)) + len(_bits(mr))
+    groups = {}
+    for d in cores:
+        if d != core:
+            groups.setdefault(_stat_mask(topo, cores, core, d), []).append(d)
+    trs = []
+    for m in sorted(groups):
+        ds = groups[m]
+        trs.append(RemoteDMATransfer(dst_ids=[dst(d) for d in ds], dma_engine_mask=m, remote_sem=S.gs,
+                                     srcs=[own], dsts=[own for d in ds]))
+        loc_n += len(_bits(m))
+    g.wait_ge(S.vs, part_done)
+    g.remote_dma_fused(trs, local_sem=S.loc)
+    g.wait_ge(S.loc, loc_n)

@@ -4,40 +4,37 @@ from concourse.mybir import AluOpType
 N = 6
 W = 1024
 CW = 256
-ORDER = [1, 2, 0, 3]
-PIECE = {1: (CW - 2, 2 * CW + 2), 2: (2 * CW + 2, 3 * CW + 2), 0: (0, CW - 2), 3: (3 * CW + 2, W)}
+NB = 4
 
 SCRATCH = {
-    "U": ("sbuf", [128, W + 4], "float32"),
-    "B": ("sbuf", [128, W], "float32"),
+    "U4": ("sbuf", [128, NB, CW + 4], "float32"),
+    "B4": ("sbuf", [128, NB, CW], "float32"),
     "EB": ("sbuf", [128, 4], "float32"),
-    "Q": ("sbuf", [128, W], "float32"),
-    "E": ("sbuf", [128, W], "float32"),
-    "SQ": ("sbuf", [128, W], "float32"),
-    "Y": ("sbuf", [128, W], "float32"),
+    "Q4": ("sbuf", [128, NB, CW], "float32"),
+    "E4": ("sbuf", [128, NB, CW], "float32"),
+    "SQ4": ("sbuf", [128, NB, CW], "float32"),
+    "Y4": ("sbuf", [128, NB, CW], "float32"),
+    "AB": ("sbuf", [128, 2, CW], "float32"),
+    "M1": ("sbuf", [128, 2, CW], "float32"),
+    "TR": ("sbuf", [128, 512], "float32"),
     "Z": ("sbuf", [128, 1057], "float32"),
     "I4": ("sbuf", [128, 128], "float32"),
     "I8": ("sbuf", [128, 128], "float32"),
-    "ONES": ("sbuf", [128, 1], "float32"),
     "KS": ("sbuf", [128, 1], "float32"),
-    "MA": ("sbuf", [128, 128], "float32"),
-    "MI": ("sbuf", [128, 128], "float32"),
     "STS": ("sbuf", [128, 128], "float32"),
-    "TA": ("sbuf", [128, 64], "float32"),
-    "TR": ("sbuf", [128, 128], "float32"),
     "G": ("sbuf", [128, 4 * N], "float32"),
     "T1": ("sbuf", [128, 8], "float32"),
     "T2": ("sbuf", [128, 2], "float32"),
     "SO": ("sbuf", [128, 2], "float32"),
-    "R0": ("psum", [128, 512], "float32"),
-    "R1": ("psum", [128, 512], "float32"),
-    "R2": ("psum", [128, 512], "float32"),
-    "R3": ("psum", [128, 512], "float32"),
-    "TC": ("psum", [128, 512], "float32"),
+    "RA": ("psum", [128, 2, CW], "float32"),
+    "RB": ("psum", [128, 2, CW], "float32"),
+    "TA": ("psum", [128, 2, CW], "float32"),
+    "TB": ("psum", [128, 2, CW], "float32"),
+    "CN": ("psum", [128, 2, CW], "float32"),
     "ST": ("psum", [128, 512], "float32"),
     "ZP": ("psum", [128, 512], "float32"),
 }
-SEMAPHORES = ["vs", "se", "su0", "su1", "su2", "su3", "sb0", "sb1", "sb2", "sb3", "sfr", "tr0", "tr1", "tr2", "tr3",
+SEMAPHORES = ["vs", "se", "su0", "su1", "su2", "su3", "sb0", "sb1", "sb2", "sb3", "sfr", "tra", "trb",
               "tst", "tfin", "hal", "gs", "loc", "sy1", "sy2", "ss"]
 
 
@@ -84,12 +81,11 @@ def rank_program(g, core, T, topo):
     cores = list(T.cores)
     v, te, sq_, sc = g.vector, g.tensor, g.sync, g.scalar
     S = T.sem
-    ADD, SUB, MUL, MAX, MIN = AluOpType.add, AluOpType.subtract, AluOpType.mult, AluOpType.max, AluOpType.min
-    R = [T.R0, T.R1, T.R2, T.R3]
+    ADD, MUL, MAX = AluOpType.add, AluOpType.mult, AluOpType.max
     su = [S.su0, S.su1, S.su2, S.su3]
     sb = [S.sb0, S.sb1, S.sb2, S.sb3]
-    tr = [S.tr0, S.tr1, S.tr2, S.tr3]
     left, right = cores[(r - 1) % N], cores[(r + 1) % N]
+    MID, EDGE = slice(1, 3), slice(0, 4, 3)
 
     n = [0]
 
@@ -109,80 +105,64 @@ def rank_program(g, core, T, topo):
         n[0] += 1
         return n[0]
 
-    def Us(c, s):
-        return T.U[:, c * CW + 2 + s:c * CW + 2 + s + CW]
+    def cp(out, a):
+        vw()
+        v.tensor_copy(out, a).then_inc(S.vs, 1)
+        n[0] += 1
+        return n[0]
 
-    def blk(t, c):
-        return t[:, c * CW:(c + 1) * CW]
+    def Us(sel, s):
+        return T.U4[:, sel, 2 + s:2 + s + CW]
 
     ms(T.Z[0:1, :], 0.0)
     ms(T.Z[0:1, 0:1057:33], 4.0)
     z_done = ms(T.I4[:], 0.0)
-    ms(T.ZP[:, 320:448], -2.0)
-    C = T.TC[:, 256:512]
-    ms(C, 0.125)
-    ms(T.ZP[:, 0:128], 0.0)
-    ms(T.MA[:], 0.0)
-    ms(T.MI[:], 0.0)
-    ms(T.ONES[:], 1.0)
-    ms(T.KS[:], 1.0 / (32.0 * N * W))
-    t = T.TC[:, 0:CW]
-    i8_done = 0
-    for c in (1, 2):
-        v.wait_ge(su[c], 16)
-        tt(t, Us(c, -2), Us(c, -1), ADD)
-        tt(t, t, Us(c, 1), ADD)
-        tt(blk(T.Q, c), t, Us(c, 2), ADD)
-        if c == 1:
-            v.wait_ge(S.sfr, 64)
-            i8_done = tt(T.I8[:], T.I4[:], T.ZP[:, 320:448], MUL)
-
-    sq_done = {}
+    ms(T.ZP[:, 0:128], -2.0)
+    ms(T.CN[:], -1.0)
+    ms(T.KS[:], -1.0 / (256.0 * N * W))
     hal_n = (len(_bits(_halo_masks(topo, cores, left, cores[(r - 2) % N], core)[1]))
              + len(_bits(_halo_masks(topo, cores, right, core, cores[(r + 2) % N])[0])))
+    v.wait_ge(su[1], 16)
+    v.wait_ge(su[2], 16)
+    tt(T.TA[:], Us(MID, -2), Us(MID, -1), ADD)
+    v.wait_ge(S.sfr, 64)
+    i8_done = tt(T.I8[:], T.I4[:], T.ZP[:, 0:128], MUL)
+    tt(T.TA[:], T.TA[:], Us(MID, 1), ADD)
+    tt(T.Q4[:, MID, :], T.TA[:], Us(MID, 2), ADD)
+    v.wait_ge(su[0], 16)
+    v.wait_ge(su[3], 16)
+    v.wait_ge(S.hal, hal_n)
+    tt(T.TB[:], Us(EDGE, -2), Us(EDGE, -1), ADD)
+    tt(T.TB[:], T.TB[:], Us(EDGE, 1), ADD)
+    tt(T.Q4[:, EDGE, :], T.TB[:], Us(EDGE, 2), ADD)
 
-    def phase2(c, shifts=None):
-        Rc = R[c][:, 0:CW]
-        v.wait_ge(tr[c], 1)
-        if shifts is None:
-            tt(blk(T.E, c), blk(T.Q, c), Rc, ADD)
-        else:
-            v.wait_ge(su[c], 16)
-            tt(Rc, Rc, Us(c, shifts[0]), ADD)
-            tt(Rc, Rc, Us(c, shifts[1]), ADD)
-            v.wait_ge(S.hal, hal_n)
-            tt(Rc, Rc, Us(c, shifts[2]), ADD)
-            tt(blk(T.E, c), Rc, Us(c, shifts[3]), ADD)
-        tt(Rc, blk(T.E, c), C, MUL)
-        sq_done[c] = tt(blk(T.SQ, c), Rc, blk(T.E, c), MUL)
-        for h in (0, 1):
-            tt(T.MA[:], T.MA[:], R[c][:, 128 * h:128 * h + 128], MAX)
-            tt(T.MI[:], T.MI[:], R[c][:, 128 * h:128 * h + 128], MIN)
+    def phase2(sel, Rp, sem, aout):
+        v.wait_ge(sem, 2)
+        tt(T.E4[:, sel, :], T.Q4[:, sel, :], Rp[:], ADD)
+        tt(Rp[:], T.E4[:, sel, :], T.CN[:], MUL)
+        done = tt(T.SQ4[:, sel, :], Rp[:], T.E4[:, sel, :], MUL)
+        tt(aout, T.E4[:, sel, :], Rp[:], MAX)
+        return done
 
-    phase2(1)
-    phase2(2)
-    phase2(0, (1, 2, -1, -2))
-    phase2(3, (-1, -2, 1, 2))
-    tt(T.ZP[:, 128:256], T.ZP[:, 0:128], T.MI[:], SUB)
-    tt(T.ZP[:, 256:320], T.MA[:, 0:64], T.ZP[:, 128:192], MAX)
-    tt(T.TA[:], T.MA[:, 64:128], T.ZP[:, 192:256], MAX)
+    sq_a = phase2(MID, T.RA, S.tra, T.TA[:])
+    sq_b = phase2(EDGE, T.RB, S.trb, T.AB[:])
+    tt(T.M1[:], T.TA[:], T.AB[:], MAX)
+    tt(T.TR[:, 0:256], T.M1[:, 0, :], T.M1[:, 1, :], MAX)
     v.wait_ge(S.tst, 1)
-    vw()
-    v.tensor_copy(T.STS[:], T.ST[:, 0:128]).then_inc(S.vs, 1)
-    n[0] += 1
-    sts_done = n[0]
-    tt(T.TR[:, 0:64], T.ZP[:, 256:320], T.TA[:], MAX)
-    o, w = 0, 32
+    sts_done = cp(T.STS[:], T.ST[:, 0:128])
+    o, w = 0, 128
     while w >= 2:
         tt(T.TR[:, o + 2 * w:o + 3 * w], T.TR[:, o:o + w], T.TR[:, o + w:o + 2 * w], MAX)
         o, w = o + 2 * w, w // 2
     own = T.G[:, 4 * r:4 * r + 2]
     tt(T.G[:, 4 * r + 1:4 * r + 2], T.TR[:, o:o + 1], T.TR[:, o + 1:o + 2], MAX)
     v.wait_ge(S.tfin, 1)
-    part_done = tt(T.G[:, 4 * r:4 * r + 1], T.ST[:, 128:129], T.KS[:], MUL)
-    y_done = {}
-    for c in ORDER:
-        y_done[c] = tt(blk(T.Y, c), R[c][:, 0:CW], Us(c, 0), ADD)
+    part_done = cp(T.G[:, 4 * r:4 * r + 1], T.ST[:, 128:129])
+    ms(T.TB[:], 0.125)
+    tt(T.RA[:], T.E4[:, MID, :], T.TB[:], MUL)
+    y_a = tt(T.Y4[:, MID, :], T.RA[:], Us(MID, 0), ADD)
+    tt(T.RB[:], T.E4[:, EDGE, :], T.TB[:], MUL)
+    y_b = tt(T.Y4[:, EDGE, :], T.RB[:], Us(EDGE, 0), ADD)
     g_n = 0
     for d in cores:
         if d != core:
@@ -193,61 +173,59 @@ def rank_program(g, core, T, topo):
     tt(T.T2[:, 0:1], T.T1[:, 0:1], T.T1[:, 1:2], ADD)
     tt(T.T2[:, 1:2], T.T1[:, 4:5], T.T1[:, 5:6], MAX)
     tt(T.SO[:, 0:1], T.T2[:, 0:1], T.T1[:, 2:3], ADD)
-    all_done = tt(T.SO[:, 1:2], T.T2[:, 1:2], T.T1[:, 6:7], MAX)
+    tt(T.T2[:, 1:2], T.T2[:, 1:2], T.T1[:, 6:7], MAX)
+    all_done = tt(T.SO[:, 1:2], T.T2[:, 1:2], T.TB[:, 0, 0:1], MUL)
 
     te.wait_ge(S.sfr, 64)
 
-    def seed(c):
-        te.wait_ge(sb[c], 16)
-        te.wait_ge(su[c], 16)
-        te.matmul(R[c][:, 0:CW], T.I4[:], blk(T.B, c), True, False)
+    def seed(k, out, sem):
+        te.wait_ge(sb[k], 16)
+        te.wait_ge(su[k], 16)
+        te.matmul(out, T.I4[:], T.B4[:, k, :], True, False)
         te.wait_ge(S.vs, i8_done)
-        te.matmul(R[c][:, 0:CW], T.I8[:], Us(c, 0), False, True).then_inc(tr[c], 1)
+        te.matmul(out, T.I8[:], T.U4[:, k, 2:2 + CW], False, True).then_inc(sem, 1)
 
-    def sums(c, first, last):
-        te.wait_ge(S.vs, sq_done[c])
-        for h in (0, 1):
-            m = te.matmul(T.ST[:, 0:128], T.SQ[:, c * CW + 128 * h:c * CW + 128 * h + 128], T.I4[:],
-                          first and h == 0, last and h == 1)
-            if last and h == 1:
-                m.then_inc(S.tst, 1)
+    def sums(ks, mark, first, last):
+        te.wait_ge(S.vs, mark)
+        for i, k in enumerate(ks):
+            for h in (0, 1):
+                m = te.matmul(T.ST[:, 0:128], T.SQ4[:, k, 128 * h:128 * h + 128], T.I4[:],
+                              first and i == 0 and h == 0, last and i == 1 and h == 1)
+                if last and i == 1 and h == 1:
+                    m.then_inc(S.tst, 1)
 
-    seed(1)
-    seed(2)
-    seed(0)
-    sums(1, True, False)
-    seed(3)
-    sums(2, False, False)
-    sums(0, False, False)
-    sums(3, False, True)
+    seed(1, T.RA[:, 0, :], S.tra)
+    seed(2, T.RA[:, 1, :], S.tra)
+    seed(0, T.RB[:, 0, :], S.trb)
+    seed(3, T.RB[:, 1, :], S.trb)
+    sums((1, 2), sq_a, True, False)
+    sums((0, 3), sq_b, False, True)
     te.wait_ge(S.vs, sts_done)
-    te.matmul(T.ST[:, 128:129], T.STS[:], T.ONES[:], True, True).then_inc(S.tfin, 1)
+    te.matmul(T.ST[:, 128:129], T.STS[:], T.KS[:], True, True).then_inc(S.tfin, 1)
 
-    def load_u(q, c):
-        a, b = PIECE[c]
-        q.dma_start(T.U[:, a + 2:b + 2], T.u[:, a:b]).then_inc(su[c], 16)
+    def load_u(q, k):
+        lo, hi = max(0, CW * k - 2), min(W, CW * k + CW + 2)
+        q.dma_start(T.U4[:, k, lo - (CW * k - 2):hi - (CW * k - 2)], T.u[:, lo:hi]).then_inc(su[k], 16)
 
-    def load_b(q, c):
-        q.dma_start(blk(T.B, c), blk(T.b, c)).then_inc(sb[c], 16)
+    def load_b(q, k):
+        q.dma_start(T.B4[:, k, :], T.b[:, CW * k:CW * k + CW]).then_inc(sb[k], 16)
 
     sq_.dma_start(T.EB[:, 0:2], T.u[:, 0:2]).then_inc(S.se, 16)
     sq_.dma_start(T.EB[:, 2:4], T.u[:, W - 2:W]).then_inc(S.se, 16)
-    load_u(sq_, 1)
-    load_b(sq_, 1)
-    load_u(sq_, 2)
-    load_u(sq_, 0)
-    load_u(sq_, 3)
+    for k in (1, 2, 0, 3):
+        load_u(sq_, k)
+    load_b(sc, 1)
+    load_b(sc, 2)
     sc.wait_ge(S.vs, z_done)
     sc.dma_start(T.I4[0:33, 0:32], T.Z[0:1, 0:1056]).then_inc(S.sfr, 16)
     for k in (1, 2, 3):
         sc.dma_start(T.I4[32 * k - 1:32 * k + 32, 32 * k:32 * k + 32], T.Z[0:1, 1:1057]).then_inc(S.sfr, 16)
-    load_b(sc, 2)
     load_b(sc, 0)
     load_b(sc, 3)
-    for k, c in enumerate(ORDER):
-        q, sem = ((sq_, S.sy1), (sc, S.sy2))[k % 2]
-        q.wait_ge(S.vs, y_done[c])
-        q.dma_start(blk(T.y, c), blk(T.Y, c)).then_inc(sem, 16)
+    for q, sem, ks in ((sq_, S.sy1, (1, 0)), (sc, S.sy2, (2, 3))):
+        for k, mark in zip(ks, (y_a, y_b)):
+            q.wait_ge(S.vs, mark)
+            q.dma_start(T.y[:, CW * k:CW * k + CW], T.Y4[:, k, :]).then_inc(sem, 16)
     sq_.wait_ge(S.vs, all_done)
     sq_.dma_start(T.s[:], T.SO[:]).then_inc(S.ss, 16)
     sq_.wait_ge(S.sy1, 32)
@@ -261,8 +239,9 @@ def rank_program(g, core, T, topo):
     ml, mr = _halo_masks(topo, cores, core, left, right)
     g.wait_ge(S.se, 32)
     g.remote_dma_fused([
-        RemoteDMATransfer(dst_ids=[dst(left)], dma_engine_mask=ml, remote_sem=S.hal, src=T.EB[:, 0:2], dst=T.U[:, W + 2:W + 4]),
-        RemoteDMATransfer(dst_ids=[dst(right)], dma_engine_mask=mr, remote_sem=S.hal, src=T.EB[:, 2:4], dst=T.U[:, 0:2]),
+        RemoteDMATransfer(dst_ids=[dst(left)], dma_engine_mask=ml, remote_sem=S.hal, src=T.EB[:, 0:2],
+                          dst=T.U4[:, NB - 1, CW + 2:CW + 4]),
+        RemoteDMATransfer(dst_ids=[dst(right)], dma_engine_mask=mr, remote_sem=S.hal, src=T.EB[:, 2:4], dst=T.U4[:, 0, 0:2]),
     ], local_sem=S.loc)
     loc_n = len(_bits(ml)) + len(_bits(mr))
     groups = {}

@@ -93,8 +93,9 @@ def rank_program(g, core, T, topo):
         if n[0]:
             v.wait_ge(S.vs, n[0])
 
-    def tt(out, a, b, op):
-        vw()
+    def tt(out, a, b, op, free=False):
+        if not free:
+            vw()
         v.tensor_tensor(out, a, b, op).then_inc(S.vs, 1)
         n[0] += 1
         return n[0]
@@ -105,8 +106,9 @@ def rank_program(g, core, T, topo):
         n[0] += 1
         return n[0]
 
-    def cp(out, a):
-        vw()
+    def cp(out, a, free=False):
+        if not free:
+            vw()
         v.tensor_copy(out, a).then_inc(S.vs, 1)
         n[0] += 1
         return n[0]
@@ -132,7 +134,7 @@ def rank_program(g, core, T, topo):
     v.wait_ge(su[0], 16)
     v.wait_ge(su[3], 16)
     v.wait_ge(S.hal, hal_n)
-    tt(T.TB[:], Us(EDGE, -2), Us(EDGE, -1), ADD)
+    tt(T.TB[:], Us(EDGE, -2), Us(EDGE, -1), ADD, True)
     tt(T.TB[:], T.TB[:], Us(EDGE, 1), ADD)
     tt(T.Q4[:, EDGE, :], T.TB[:], Us(EDGE, 2), ADD)
 
@@ -140,16 +142,15 @@ def rank_program(g, core, T, topo):
         v.wait_ge(sem, 2)
         tt(T.E4[:, sel, :], T.Q4[:, sel, :], Rp[:], ADD)
         tt(Rp[:], T.E4[:, sel, :], T.CN[:], MUL)
-        done = tt(T.SQ4[:, sel, :], Rp[:], T.E4[:, sel, :], MUL)
-        tt(aout, T.E4[:, sel, :], Rp[:], MAX)
-        return done
+        tt(T.SQ4[:, sel, :], Rp[:], T.E4[:, sel, :], MUL)
+        return tt(aout, T.E4[:, sel, :], Rp[:], MAX, True)
 
     sq_a = phase2(MID, T.RA, S.tra, T.TA[:])
     sq_b = phase2(EDGE, T.RB, S.trb, T.AB[:])
     tt(T.M1[:], T.TA[:], T.AB[:], MAX)
     tt(T.TR[:, 0:256], T.M1[:, 0, :], T.M1[:, 1, :], MAX)
     v.wait_ge(S.tst, 1)
-    sts_done = cp(T.STS[:], T.ST[:, 0:128])
+    sts_done = cp(T.STS[:], T.ST[:, 0:128], True)
     o, w = 0, 128
     while w >= 2:
         tt(T.TR[:, o + 2 * w:o + 3 * w], T.TR[:, o:o + w], T.TR[:, o + w:o + 2 * w], MAX)
@@ -157,7 +158,7 @@ def rank_program(g, core, T, topo):
     own = T.G[:, 4 * r:4 * r + 2]
     tt(T.G[:, 4 * r + 1:4 * r + 2], T.TR[:, o:o + 1], T.TR[:, o + 1:o + 2], MAX)
     v.wait_ge(S.tfin, 1)
-    part_done = cp(T.G[:, 4 * r:4 * r + 1], T.ST[:, 128:129])
+    part_done = cp(T.G[:, 4 * r:4 * r + 1], T.ST[:, 128:129], True)
     ms(T.TB[:], 0.125)
     tt(T.RA[:], T.E4[:, MID, :], T.TB[:], MUL)
     y_a = tt(T.Y4[:, MID, :], T.RA[:], Us(MID, 0), ADD)
@@ -169,12 +170,12 @@ def rank_program(g, core, T, topo):
             g_n += len(_bits(_stat_mask(topo, cores, d, core)))
     v.wait_ge(S.gs, g_n)
     tt(T.T1[:, 0:3], T.G[:, 0:12:4], T.G[:, 12:24:4], ADD)
-    tt(T.T1[:, 4:7], T.G[:, 1:12:4], T.G[:, 13:24:4], MAX)
+    tt(T.T1[:, 4:7], T.G[:, 1:12:4], T.G[:, 13:24:4], MAX, True)
     tt(T.T2[:, 0:1], T.T1[:, 0:1], T.T1[:, 1:2], ADD)
-    tt(T.T2[:, 1:2], T.T1[:, 4:5], T.T1[:, 5:6], MAX)
+    tt(T.T2[:, 1:2], T.T1[:, 4:5], T.T1[:, 5:6], MAX, True)
     tt(T.SO[:, 0:1], T.T2[:, 0:1], T.T1[:, 2:3], ADD)
-    tt(T.T2[:, 1:2], T.T2[:, 1:2], T.T1[:, 6:7], MAX)
-    all_done = tt(T.SO[:, 1:2], T.T2[:, 1:2], T.TB[:, 0, 0:1], MUL)
+    tt(T.T1[:, 7:8], T.T2[:, 1:2], T.T1[:, 6:7], MAX, True)
+    all_done = tt(T.SO[:, 1:2], T.T1[:, 7:8], T.TB[:, 0, 0:1], MUL)
 
     te.wait_ge(S.sfr, 64)
 

@@ -34,7 +34,7 @@ SCRATCH = {
     "ST": ("psum", [128, 512], "float32"),
     "ZP": ("psum", [128, 512], "float32"),
 }
-SEMAPHORES = ["vs", "se", "su0", "su1", "su2", "su3", "sb0", "sb1", "sb2", "sb3", "sfr", "tra", "trb",
+SEMAPHORES = ["vs", "v0", "v1", "v2", "v3", "se", "su0", "su1", "su2", "su3", "sb0", "sb1", "sb2", "sb3", "sfr", "tra", "trb",
               "tst", "tfin", "hal", "gs", "loc", "sy1", "sy2", "ss"]
 
 
@@ -100,8 +100,9 @@ def rank_program(g, core, T, topo):
         n[0] += 1
         return n[0]
 
-    def ms(ap, c):
-        vw()
+    def ms(ap, c, free=False):
+        if not free:
+            vw()
         v.memset(ap, c).then_inc(S.vs, 1)
         n[0] += 1
         return n[0]
@@ -113,40 +114,59 @@ def rank_program(g, core, T, topo):
         n[0] += 1
         return n[0]
 
+    vk = [S.v0, S.v1, S.v2, S.v3]
+    nk = [0, 0, 0, 0]
+
+    def bt(k, out, a, b, op):
+        if nk[k]:
+            v.wait_ge(vk[k], nk[k])
+        v.tensor_tensor(out, a, b, op).then_inc(vk[k], 1)
+        nk[k] += 1
+        return nk[k]
+
     def Us(sel, s):
         return T.U4[:, sel, 2 + s:2 + s + CW]
 
     ms(T.Z[0:1, :], 0.0)
-    ms(T.Z[0:1, 0:1057:33], 4.0)
-    z_done = ms(T.I4[:], 0.0)
+    ms(T.I4[:], 0.0, True)
+    z_done = ms(T.Z[0:1, 0:1057:33], 4.0)
     ms(T.ZP[:, 0:128], -2.0)
-    ms(T.CN[:], -1.0)
-    ms(T.KS[:], -1.0 / (256.0 * N * W))
+    ms(T.CN[:], -1.0, True)
+    ms(T.KS[:], -1.0 / (256.0 * N * W), True)
     hal_n = (len(_bits(_halo_masks(topo, cores, left, cores[(r - 2) % N], core)[1]))
              + len(_bits(_halo_masks(topo, cores, right, core, cores[(r + 2) % N])[0])))
-    v.wait_ge(su[1], 16)
-    v.wait_ge(su[2], 16)
-    tt(T.TA[:], Us(MID, -2), Us(MID, -1), ADD)
-    v.wait_ge(S.sfr, 64)
-    i8_done = tt(T.I8[:], T.I4[:], T.ZP[:, 0:128], MUL)
-    tt(T.TA[:], T.TA[:], Us(MID, 1), ADD)
-    tt(T.Q4[:, MID, :], T.TA[:], Us(MID, 2), ADD)
-    v.wait_ge(su[0], 16)
-    v.wait_ge(su[3], 16)
-    v.wait_ge(S.hal, hal_n)
-    tt(T.TB[:], Us(EDGE, -2), Us(EDGE, -1), ADD, True)
-    tt(T.TB[:], T.TB[:], Us(EDGE, 1), ADD)
-    tt(T.Q4[:, EDGE, :], T.TB[:], Us(EDGE, 2), ADD)
-
-    def phase2(sel, Rp, sem, aout):
+    TMP = {1: T.TA[:, 0, :], 2: T.TA[:, 1, :], 0: T.TB[:, 0, :], 3: T.TB[:, 1, :]}
+    RP = {1: T.RA[:, 0, :], 2: T.RA[:, 1, :], 0: T.RB[:, 0, :], 3: T.RB[:, 1, :]}
+    AO = {1: T.TA[:, 0, :], 2: T.TA[:, 1, :], 0: T.AB[:, 0, :], 3: T.AB[:, 1, :]}
+    SH = {0: (1, 2, -1, -2), 1: (-2, -1, 1, 2), 2: (-2, -1, 1, 2), 3: (-2, -1, 1, 2)}
+    i8_done = 0
+    for pair in ((1, 2), (0, 3)):
+        for k in pair:
+            v.wait_ge(su[k], 16)
+            bt(k, TMP[k], Us(k, SH[k][0]), Us(k, SH[k][1]), ADD)
+        if pair[0] == 1:
+            v.wait_ge(S.sfr, 64)
+            i8_done = tt(T.I8[:], T.I4[:], T.ZP[:, 0:128], MUL)
+        else:
+            v.wait_ge(S.hal, hal_n)
+        for k in pair:
+            bt(k, TMP[k], TMP[k], Us(k, SH[k][2]), ADD)
+        for k in pair:
+            bt(k, T.Q4[:, k, :], TMP[k], Us(k, SH[k][3]), ADD)
+    sq_done = {}
+    for pair, sem in (((1, 2), S.tra), ((0, 3), S.trb)):
         v.wait_ge(sem, 2)
-        tt(T.E4[:, sel, :], T.Q4[:, sel, :], Rp[:], ADD)
-        tt(Rp[:], T.E4[:, sel, :], T.CN[:], MUL)
-        tt(T.SQ4[:, sel, :], Rp[:], T.E4[:, sel, :], MUL)
-        return tt(aout, T.E4[:, sel, :], Rp[:], MAX, True)
-
-    sq_a = phase2(MID, T.RA, S.tra, T.TA[:])
-    sq_b = phase2(EDGE, T.RB, S.trb, T.AB[:])
+        for k in pair:
+            bt(k, T.E4[:, k, :], T.Q4[:, k, :], RP[k], ADD)
+        vw()
+        for k in pair:
+            bt(k, RP[k], T.E4[:, k, :], T.CN[:, 0, :], MUL)
+        for k in pair:
+            sq_done[k] = bt(k, T.SQ4[:, k, :], RP[k], T.E4[:, k, :], MUL)
+        for k in pair:
+            bt(k, AO[k], T.E4[:, k, :], RP[k], MAX)
+    for k in range(NB):
+        v.wait_ge(vk[k], nk[k])
     tt(T.M1[:], T.TA[:], T.AB[:], MAX)
     tt(T.TR[:, 0:256], T.M1[:, 0, :], T.M1[:, 1, :], MAX)
     v.wait_ge(S.tst, 1)
@@ -161,9 +181,9 @@ def rank_program(g, core, T, topo):
     part_done = cp(T.G[:, 4 * r:4 * r + 1], T.ST[:, 128:129], True)
     ms(T.TB[:], 0.125)
     tt(T.RA[:], T.E4[:, MID, :], T.TB[:], MUL)
-    y_a = tt(T.Y4[:, MID, :], T.RA[:], Us(MID, 0), ADD)
-    tt(T.RB[:], T.E4[:, EDGE, :], T.TB[:], MUL)
-    y_b = tt(T.Y4[:, EDGE, :], T.RB[:], Us(EDGE, 0), ADD)
+    tt(T.RB[:], T.E4[:, EDGE, :], T.TB[:], MUL, True)
+    tt(T.Y4[:, MID, :], T.RA[:], Us(MID, 0), ADD)
+    y_done = tt(T.Y4[:, EDGE, :], T.RB[:], Us(EDGE, 0), ADD, True)
     g_n = 0
     for d in cores:
         if d != core:
@@ -179,28 +199,28 @@ def rank_program(g, core, T, topo):
 
     te.wait_ge(S.sfr, 64)
 
-    def seed(k, out, sem):
+    def seed(k, sem):
         te.wait_ge(sb[k], 16)
         te.wait_ge(su[k], 16)
-        te.matmul(out, T.I4[:], T.B4[:, k, :], True, False)
+        te.matmul(RP[k], T.I4[:], T.B4[:, k, :], True, False)
         te.wait_ge(S.vs, i8_done)
-        te.matmul(out, T.I8[:], T.U4[:, k, 2:2 + CW], False, True).then_inc(sem, 1)
+        te.matmul(RP[k], T.I8[:], T.U4[:, k, 2:2 + CW], False, True).then_inc(sem, 1)
 
-    def sums(ks, mark, first, last):
-        te.wait_ge(S.vs, mark)
+    def sums(ks, first, last):
         for i, k in enumerate(ks):
+            te.wait_ge(vk[k], sq_done[k])
             for h in (0, 1):
                 m = te.matmul(T.ST[:, 0:128], T.SQ4[:, k, 128 * h:128 * h + 128], T.I4[:],
                               first and i == 0 and h == 0, last and i == 1 and h == 1)
                 if last and i == 1 and h == 1:
                     m.then_inc(S.tst, 1)
 
-    seed(1, T.RA[:, 0, :], S.tra)
-    seed(2, T.RA[:, 1, :], S.tra)
-    seed(0, T.RB[:, 0, :], S.trb)
-    seed(3, T.RB[:, 1, :], S.trb)
-    sums((1, 2), sq_a, True, False)
-    sums((0, 3), sq_b, False, True)
+    seed(1, S.tra)
+    seed(2, S.tra)
+    seed(0, S.trb)
+    seed(3, S.trb)
+    sums((1, 2), True, False)
+    sums((0, 3), False, True)
     te.wait_ge(S.vs, sts_done)
     te.matmul(T.ST[:, 128:129], T.STS[:], T.KS[:], True, True).then_inc(S.tfin, 1)
 
@@ -224,8 +244,8 @@ def rank_program(g, core, T, topo):
     load_b(sc, 0)
     load_b(sc, 3)
     for q, sem, ks in ((sq_, S.sy1, (1, 0)), (sc, S.sy2, (2, 3))):
-        for k, mark in zip(ks, (y_a, y_b)):
-            q.wait_ge(S.vs, mark)
+        q.wait_ge(S.vs, y_done)
+        for k in ks:
             q.dma_start(T.y[:, CW * k:CW * k + CW], T.Y4[:, k, :]).then_inc(sem, 16)
     sq_.wait_ge(S.vs, all_done)
     sq_.dma_start(T.s[:], T.SO[:]).then_inc(S.ss, 16)

@@ -1,5 +1,6 @@
+import math
 from concourse.bass import DstId, RemoteDMATransfer
-from concourse.mybir import AluOpType
+from concourse.mybir import AluOpType, AxisListType, ActivationFunctionType
 
 N = 6
 W = 1024
@@ -10,32 +11,23 @@ SCRATCH = {
     "U4": ("sbuf", [128, NB, CW + 4], "float32"),
     "B4": ("sbuf", [128, NB, CW], "float32"),
     "EB": ("sbuf", [128, 4], "float32"),
-    "Q4": ("sbuf", [128, NB, CW], "float32"),
-    "E4": ("sbuf", [128, NB, CW], "float32"),
-    "SQ4": ("sbuf", [128, NB, CW], "float32"),
+    "P4": ("sbuf", [128, NB, CW + 4], "float32"),
     "Y4": ("sbuf", [128, NB, CW], "float32"),
-    "AB": ("sbuf", [128, 2, CW], "float32"),
-    "M1": ("sbuf", [128, 2, CW], "float32"),
-    "TR": ("sbuf", [128, 512], "float32"),
-    "Z": ("sbuf", [128, 1057], "float32"),
-    "I4": ("sbuf", [128, 128], "float32"),
-    "I8": ("sbuf", [128, 128], "float32"),
-    "KS": ("sbuf", [128, 1], "float32"),
-    "STS": ("sbuf", [128, 128], "float32"),
-    "G": ("sbuf", [128, 4 * N], "float32"),
-    "T1": ("sbuf", [128, 8], "float32"),
-    "T2": ("sbuf", [128, 2], "float32"),
+    "D4": ("sbuf", [128, NB, CW], "float32"),
+    "SQ4": ("sbuf", [128, NB, CW], "float32"),
+    "G": ("sbuf", [128, 8 * N], "float32"),
     "SO": ("sbuf", [128, 2], "float32"),
-    "RA": ("psum", [128, 2, CW], "float32"),
-    "RB": ("psum", [128, 2, CW], "float32"),
-    "TA": ("psum", [128, 2, CW], "float32"),
-    "TB": ("psum", [128, 2, CW], "float32"),
-    "CN": ("psum", [128, 2, CW], "float32"),
-    "ST": ("psum", [128, 512], "float32"),
-    "ZP": ("psum", [128, 512], "float32"),
+    "UP0": ("psum", [128, 512], "float32"),
+    "UP1": ("psum", [128, 512], "float32"),
+    "UP2": ("psum", [128, 512], "float32"),
+    "UP3": ("psum", [128, 512], "float32"),
+    "PP0": ("psum", [128, 512], "float32"),
+    "PP1": ("psum", [128, 512], "float32"),
+    "PP2": ("psum", [128, 512], "float32"),
+    "PP3": ("psum", [128, 512], "float32"),
 }
-SEMAPHORES = ["vs", "v0", "v1", "v2", "v3", "se", "su0", "su1", "su2", "su3", "sb0", "sb1", "sb2", "sb3", "sfr", "tra", "trb",
-              "tst", "tfin", "hal", "gs", "loc", "sy1", "sy2", "ss"]
+SEMAPHORES = ["c0", "c1", "c2", "c3", "cb0", "cb1", "cb2", "cb3", "su0", "su1", "su2", "su3", "sb0", "sb1", "sb2", "sb3",
+              "se", "hal", "vh", "gs", "loc", "sy", "vf", "ss"]
 
 
 def _bits(m):
@@ -79,150 +71,25 @@ def rank_program(g, core, T, topo):
     if r is None:
         return
     cores = list(T.cores)
-    v, te, sq_, sc = g.vector, g.tensor, g.sync, g.scalar
+    v, sq_, sc = g.vector, g.sync, g.scalar
     S = T.sem
-    ADD, MUL, MAX = AluOpType.add, AluOpType.mult, AluOpType.max
+    ADD, SUB, MAX = AluOpType.add, AluOpType.subtract, AluOpType.max
+    COPY, SQUARE = ActivationFunctionType.Copy, ActivationFunctionType.Square
+    X = AxisListType.X
+    ck = [S.c0, S.c1, S.c2, S.c3]
+    cb = [S.cb0, S.cb1, S.cb2, S.cb3]
     su = [S.su0, S.su1, S.su2, S.su3]
     sb = [S.sb0, S.sb1, S.sb2, S.sb3]
+    UP = [T.UP0, T.UP1, T.UP2, T.UP3]
+    PP = [T.PP0, T.PP1, T.PP2, T.PP3]
     left, right = cores[(r - 1) % N], cores[(r + 1) % N]
-    MID, EDGE = slice(1, 3), slice(0, 4, 3)
-
-    n = [0]
-
-    def vw():
-        if n[0]:
-            v.wait_ge(S.vs, n[0])
-
-    def tt(out, a, b, op, free=False):
-        if not free:
-            vw()
-        v.tensor_tensor(out, a, b, op).then_inc(S.vs, 1)
-        n[0] += 1
-        return n[0]
-
-    def ms(ap, c, free=False):
-        if not free:
-            vw()
-        v.memset(ap, c).then_inc(S.vs, 1)
-        n[0] += 1
-        return n[0]
-
-    def cp(out, a, free=False):
-        if not free:
-            vw()
-        v.tensor_copy(out, a).then_inc(S.vs, 1)
-        n[0] += 1
-        return n[0]
-
-    vk = [S.v0, S.v1, S.v2, S.v3]
-    nk = [0, 0, 0, 0]
-
-    def bt(k, out, a, b, op):
-        if nk[k]:
-            v.wait_ge(vk[k], nk[k])
-        v.tensor_tensor(out, a, b, op).then_inc(vk[k], 1)
-        nk[k] += 1
-        return nk[k]
-
-    def Us(sel, s):
-        return T.U4[:, sel, 2 + s:2 + s + CW]
-
-    ms(T.Z[0:1, :], 0.0)
-    ms(T.I4[:], 0.0, True)
-    z_done = ms(T.Z[0:1, 0:1057:33], 4.0)
-    ms(T.ZP[:, 0:128], -2.0)
-    ms(T.CN[:], -1.0, True)
-    ms(T.KS[:], -1.0 / (256.0 * N * W), True)
-    hal_n = (len(_bits(_halo_masks(topo, cores, left, cores[(r - 2) % N], core)[1]))
-             + len(_bits(_halo_masks(topo, cores, right, core, cores[(r + 2) % N])[0])))
-    TMP = {1: T.TA[:, 0, :], 2: T.TA[:, 1, :], 0: T.TB[:, 0, :], 3: T.TB[:, 1, :]}
-    RP = {1: T.RA[:, 0, :], 2: T.RA[:, 1, :], 0: T.RB[:, 0, :], 3: T.RB[:, 1, :]}
-    AO = {1: T.TA[:, 0, :], 2: T.TA[:, 1, :], 0: T.AB[:, 0, :], 3: T.AB[:, 1, :]}
-    SH = {0: (1, 2, -1, -2), 1: (-2, -1, 1, 2), 2: (-2, -1, 1, 2), 3: (-2, -1, 1, 2)}
-    i8_done = 0
-    for pair in ((1, 2), (0, 3)):
-        for k in pair:
-            v.wait_ge(su[k], 16)
-            bt(k, TMP[k], Us(k, SH[k][0]), Us(k, SH[k][1]), ADD)
-        if pair[0] == 1:
-            v.wait_ge(S.sfr, 64)
-            i8_done = tt(T.I8[:], T.I4[:], T.ZP[:, 0:128], MUL)
-        else:
-            v.wait_ge(S.hal, hal_n)
-        for k in pair:
-            bt(k, TMP[k], TMP[k], Us(k, SH[k][2]), ADD)
-        for k in pair:
-            bt(k, T.Q4[:, k, :], TMP[k], Us(k, SH[k][3]), ADD)
-    sq_done = {}
-    for pair, sem in (((1, 2), S.tra), ((0, 3), S.trb)):
-        v.wait_ge(sem, 2)
-        for k in pair:
-            bt(k, T.E4[:, k, :], T.Q4[:, k, :], RP[k], ADD)
-        vw()
-        for k in pair:
-            bt(k, RP[k], T.E4[:, k, :], T.CN[:, 0, :], MUL)
-        for k in pair:
-            sq_done[k] = bt(k, T.SQ4[:, k, :], RP[k], T.E4[:, k, :], MUL)
-        for k in pair:
-            bt(k, AO[k], T.E4[:, k, :], RP[k], MAX)
-    for k in range(NB):
-        v.wait_ge(vk[k], nk[k])
-    tt(T.M1[:], T.TA[:], T.AB[:], MAX)
-    tt(T.TR[:, 0:256], T.M1[:, 0, :], T.M1[:, 1, :], MAX)
-    v.wait_ge(S.tst, 1)
-    sts_done = cp(T.STS[:], T.ST[:, 0:128], True)
-    o, w = 0, 128
-    while w >= 2:
-        tt(T.TR[:, o + 2 * w:o + 3 * w], T.TR[:, o:o + w], T.TR[:, o + w:o + 2 * w], MAX)
-        o, w = o + 2 * w, w // 2
-    own = T.G[:, 4 * r:4 * r + 2]
-    tt(T.G[:, 4 * r + 1:4 * r + 2], T.TR[:, o:o + 1], T.TR[:, o + 1:o + 2], MAX)
-    v.wait_ge(S.tfin, 1)
-    part_done = cp(T.G[:, 4 * r:4 * r + 1], T.ST[:, 128:129], True)
-    ms(T.TB[:], 0.125)
-    tt(T.RA[:], T.E4[:, MID, :], T.TB[:], MUL)
-    tt(T.RB[:], T.E4[:, EDGE, :], T.TB[:], MUL, True)
-    tt(T.Y4[:, MID, :], T.RA[:], Us(MID, 0), ADD)
-    y_done = tt(T.Y4[:, EDGE, :], T.RB[:], Us(EDGE, 0), ADD, True)
-    g_n = 0
-    for d in cores:
-        if d != core:
-            g_n += len(_bits(_stat_mask(topo, cores, d, core)))
-    v.wait_ge(S.gs, g_n)
-    tt(T.T1[:, 0:3], T.G[:, 0:12:4], T.G[:, 12:24:4], ADD)
-    tt(T.T1[:, 4:7], T.G[:, 1:12:4], T.G[:, 13:24:4], MAX, True)
-    tt(T.T2[:, 0:1], T.T1[:, 0:1], T.T1[:, 1:2], ADD)
-    tt(T.T2[:, 1:2], T.T1[:, 4:5], T.T1[:, 5:6], MAX, True)
-    tt(T.SO[:, 0:1], T.T2[:, 0:1], T.T1[:, 2:3], ADD)
-    tt(T.T1[:, 7:8], T.T2[:, 1:2], T.T1[:, 6:7], MAX, True)
-    all_done = tt(T.SO[:, 1:2], T.T1[:, 7:8], T.TB[:, 0, 0:1], MUL)
-
-    te.wait_ge(S.sfr, 64)
-
-    def seed(k, sem):
-        te.wait_ge(sb[k], 16)
-        te.wait_ge(su[k], 16)
-        te.matmul(RP[k], T.I4[:], T.B4[:, k, :], True, False)
-        te.wait_ge(S.vs, i8_done)
-        te.matmul(RP[k], T.I8[:], T.U4[:, k, 2:2 + CW], False, True).then_inc(sem, 1)
-
-    def sums(ks, first, last):
-        for i, k in enumerate(ks):
-            te.wait_ge(vk[k], sq_done[k])
-            for h in (0, 1):
-                m = te.matmul(T.ST[:, 0:128], T.SQ4[:, k, 128 * h:128 * h + 128], T.I4[:],
-                              first and i == 0 and h == 0, last and i == 1 and h == 1)
-                if last and i == 1 and h == 1:
-                    m.then_inc(S.tst, 1)
-
-    seed(1, S.tra)
-    seed(2, S.tra)
-    seed(0, S.trb)
-    seed(3, S.trb)
-    sums((1, 2), True, False)
-    sums((0, 3), False, True)
-    te.wait_ge(S.vs, sts_done)
-    te.matmul(T.ST[:, 128:129], T.STS[:], T.KS[:], True, True).then_inc(S.tfin, 1)
+    ORDER = (1, 2, 0, 3)
+    PLO = {0: 2, 1: 0, 2: 0, 3: 0}
+    PHI = {0: CW + 3, 1: CW + 3, 2: CW + 3, 3: CW + 1}
+    UHI = {0: CW + 3, 1: CW + 3, 2: CW + 3, 3: CW + 2}
+    OPS = {0: 3, 1: 3, 2: 3, 3: 0}
+    OSB = {0: 0, 1: 0, 2: 0, 3: 3}
+    C_UP, C_P, C_PP, C_Q, C_Y8, C_Y, C_D, C_END = 1, 2, 3, 4, 5, 6, 7, 9
 
     def load_u(q, k):
         lo, hi = max(0, CW * k - 2), min(W, CW * k + CW + 2)
@@ -233,25 +100,116 @@ def rank_program(g, core, T, topo):
 
     sq_.dma_start(T.EB[:, 0:2], T.u[:, 0:2]).then_inc(S.se, 16)
     sq_.dma_start(T.EB[:, 2:4], T.u[:, W - 2:W]).then_inc(S.se, 16)
-    for k in (1, 2, 0, 3):
-        load_u(sq_, k)
-    load_b(sc, 1)
+    load_u(sq_, 1)
+    load_u(sc, 2)
+    load_u(sq_, 0)
+    load_u(sc, 3)
+    load_b(sq_, 1)
     load_b(sc, 2)
-    sc.wait_ge(S.vs, z_done)
-    sc.dma_start(T.I4[0:33, 0:32], T.Z[0:1, 0:1056]).then_inc(S.sfr, 16)
-    for k in (1, 2, 3):
-        sc.dma_start(T.I4[32 * k - 1:32 * k + 32, 32 * k:32 * k + 32], T.Z[0:1, 1:1057]).then_inc(S.sfr, 16)
-    load_b(sc, 0)
+    load_b(sq_, 0)
     load_b(sc, 3)
-    for q, sem, ks in ((sq_, S.sy1, (1, 0)), (sc, S.sy2, (2, 3))):
-        q.wait_ge(S.vs, y_done)
-        for k in ks:
-            q.dma_start(T.y[:, CW * k:CW * k + CW], T.Y4[:, k, :]).then_inc(sem, 16)
-    sq_.wait_ge(S.vs, all_done)
+
+    def a_up(k):
+        sc.wait_ge(su[k], 16)
+        sc.activation(UP[k][:, PLO[k]:UHI[k]], T.U4[:, k, PLO[k]:UHI[k]], COPY).then_inc(ck[k], 1)
+
+    def a_pp(k):
+        sc.wait_ge(ck[k], C_P)
+        sc.activation(PP[k][:, 0:CW], T.P4[:, k, OPS[k]:OPS[k] + CW], COPY).then_inc(ck[k], 1)
+
+    def a_b(k):
+        sc.wait_ge(sb[k], 16)
+        sc.activation(T.B4[:, k, :], T.B4[:, k, :], COPY, scale=4.0).then_inc(cb[k], 1)
+
+    def a_y(k):
+        sc.wait_ge(ck[k], C_Y8)
+        sc.activation(T.Y4[:, k, :], PP[k][:, 0:CW], COPY, scale=0.125).then_inc(ck[k], 1)
+
+    def a_sq(k):
+        sc.wait_ge(ck[k], C_D)
+        sc.activation(T.SQ4[:, k, :], T.D4[:, k, :], SQUARE, scale=1.0 / math.sqrt(float(N * W)),
+                      accum_out=T.G[:, 8 * r + 2 * k:8 * r + 2 * k + 1]).then_inc(ck[k], 1)
+
+    for k in ORDER:
+        a_up(k)
+    a_pp(1)
+    a_pp(2)
+    a_b(1)
+    a_b(2)
+    a_pp(0)
+    a_pp(3)
+    a_b(0)
+    a_b(3)
+    for k in ORDER:
+        a_y(k)
+    for k in ORDER:
+        a_sq(k)
+
+    def v_p(k):
+        v.wait_ge(su[k], 16)
+        v.wait_ge(ck[k], C_UP)
+        v.tensor_tensor(T.P4[:, k, PLO[k]:PHI[k]], UP[k][:, PLO[k]:PHI[k]], T.U4[:, k, PLO[k] + 1:PHI[k] + 1],
+                        ADD).then_inc(ck[k], 1)
+
+    def v_q(k):
+        v.wait_ge(ck[k], C_PP)
+        v.tensor_tensor(PP[k][:, 0:CW], PP[k][:, 0:CW], T.P4[:, k, OSB[k]:OSB[k] + CW], ADD).then_inc(ck[k], 1)
+
+    def v_y8(k):
+        v.wait_ge(cb[k], 1)
+        v.wait_ge(ck[k], C_Q)
+        v.tensor_tensor(PP[k][:, 0:CW], PP[k][:, 0:CW], T.B4[:, k, :], ADD).then_inc(ck[k], 1)
+
+    def v_d(k):
+        v.wait_ge(ck[k], C_Y)
+        v.tensor_tensor(T.D4[:, k, :], T.Y4[:, k, :], UP[k][:, 2:2 + CW], SUB).then_inc(ck[k], 1)
+
+    def v_m(k):
+        v.wait_ge(ck[k], C_D)
+        v.tensor_reduce(T.G[:, 8 * r + 2 * k + 1:8 * r + 2 * k + 2], T.D4[:, k, :], X, MAX,
+                        apply_absolute_value=True).then_inc(ck[k], 1)
+
+    hal_n = (len(_bits(_halo_masks(topo, cores, left, cores[(r - 2) % N], core)[1]))
+             + len(_bits(_halo_masks(topo, cores, right, core, cores[(r + 2) % N])[0])))
+    for k in ORDER:
+        v_p(k)
+    v_q(1)
+    v_q(2)
+    v_y8(1)
+    v.wait_ge(S.hal, hal_n)
+    v.tensor_tensor(T.P4[:, 0, 0:2], T.U4[:, 0, 0:2], T.U4[:, 0, 1:3], ADD).then_inc(S.vh, 1)
+    v.tensor_tensor(T.P4[:, 3, CW + 1:CW + 3], T.U4[:, 3, CW + 1:CW + 3], T.U4[:, 3, CW + 2:CW + 4], ADD).then_inc(S.vh, 1)
+    v_y8(2)
+    v.wait_ge(S.vh, 2)
+    v_q(0)
+    v_q(3)
+    v_y8(0)
+    v_y8(3)
+    v_d(1)
+    v_d(2)
+    v_m(1)
+    v_m(2)
+    v_d(0)
+    v_d(3)
+    v_m(0)
+    v_m(3)
+    g_n = 0
+    for d in cores:
+        if d != core:
+            g_n += len(_bits(_stat_mask(topo, cores, d, core)))
+    v.wait_ge(S.gs, g_n)
+    for k in range(NB):
+        v.wait_ge(ck[k], C_END)
+    v.tensor_reduce(T.SO[:, 0:1], T.G[:, 0:8 * N:2], X, ADD).then_inc(S.vf, 1)
+    v.tensor_reduce(T.SO[:, 1:2], T.G[:, 1:8 * N:2], X, MAX).then_inc(S.vf, 1)
+
+    for k in ORDER:
+        sq_.wait_ge(ck[k], C_Y)
+        sq_.dma_start(T.y[:, CW * k:CW * k + CW], T.Y4[:, k, :]).then_inc(S.sy, 16)
+    sq_.wait_ge(S.vf, 2)
     sq_.dma_start(T.s[:], T.SO[:]).then_inc(S.ss, 16)
-    sq_.wait_ge(S.sy1, 32)
+    sq_.wait_ge(S.sy, 64)
     sq_.wait_ge(S.ss, 16)
-    sc.wait_ge(S.sy2, 32)
 
     def dst(d):
         rid, pid = topo.addr(d, core)
@@ -265,6 +223,7 @@ def rank_program(g, core, T, topo):
         RemoteDMATransfer(dst_ids=[dst(right)], dma_engine_mask=mr, remote_sem=S.hal, src=T.EB[:, 2:4], dst=T.U4[:, 0, 0:2]),
     ], local_sem=S.loc)
     loc_n = len(_bits(ml)) + len(_bits(mr))
+    own = T.G[:, 8 * r:8 * r + 8]
     groups = {}
     for d in cores:
         if d != core:
@@ -275,6 +234,7 @@ def rank_program(g, core, T, topo):
         trs.append(RemoteDMATransfer(dst_ids=[dst(d) for d in ds], dma_engine_mask=m, remote_sem=S.gs,
                                      srcs=[own], dsts=[own for d in ds]))
         loc_n += len(_bits(m))
-    g.wait_ge(S.vs, part_done)
+    for k in range(NB):
+        g.wait_ge(ck[k], C_END)
     g.remote_dma_fused(trs, local_sem=S.loc)
     g.wait_ge(S.loc, loc_n)

@@ -6,28 +6,31 @@ N = 6
 W = 1024
 CW = 256
 NB = 4
+XW = CW + 12
 
 SCRATCH = {
-    "U4": ("sbuf", [128, NB, CW + 4], "float32"),
-    "B4": ("sbuf", [128, NB, CW], "float32"),
+    "U4": ("sbuf", [128, NB, XW], "float32"),
+    "BF": ("sbuf", [128, W], "float32"),
+    "N9": ("sbuf", [128, W], "float32"),
     "EB": ("sbuf", [128, 4], "float32"),
-    "P4": ("sbuf", [128, NB, CW + 4], "float32"),
-    "Y4": ("sbuf", [128, NB, CW], "float32"),
+    "H": ("sbuf", [128, 4], "float32"),
     "D4": ("sbuf", [128, NB, CW], "float32"),
     "SQ4": ("sbuf", [128, NB, CW], "float32"),
+    "Y4": ("sbuf", [128, NB, CW], "float32"),
     "G": ("sbuf", [128, 8 * N], "float32"),
-    "SO": ("sbuf", [128, 2], "float32"),
-    "UP0": ("psum", [128, 512], "float32"),
-    "UP1": ("psum", [128, 512], "float32"),
-    "UP2": ("psum", [128, 512], "float32"),
-    "UP3": ("psum", [128, 512], "float32"),
-    "PP0": ("psum", [128, 512], "float32"),
-    "PP1": ("psum", [128, 512], "float32"),
-    "PP2": ("psum", [128, 512], "float32"),
-    "PP3": ("psum", [128, 512], "float32"),
+    "CS": ("sbuf", [128, 4 * N], "float32"),
+    "R": ("sbuf", [128, 8 * N], "float32"),
+    "SP0": ("psum", [128, 512], "float32"),
+    "SP1": ("psum", [128, 512], "float32"),
+    "SP2": ("psum", [128, 512], "float32"),
+    "SP3": ("psum", [128, 512], "float32"),
+    "DP0": ("psum", [128, 512], "float32"),
+    "DP1": ("psum", [128, 512], "float32"),
+    "DP2": ("psum", [128, 512], "float32"),
+    "DP3": ("psum", [128, 512], "float32"),
 }
-SEMAPHORES = ["c0", "c1", "c2", "c3", "cb0", "cb1", "cb2", "cb3", "su0", "su1", "su2", "su3", "sb0", "sb1", "sb2", "sb3",
-              "se", "hal", "vh", "gs", "loc", "sy", "vf", "ss"]
+SEMAPHORES = (["z", "z3", "se", "st", "vh", "hal", "gs", "loc", "sy", "vf", "ss"]
+              + [p + "%d" % k for p in ("su", "sb", "sv", "n9", "cb", "dk", "yv") for k in range(NB)])
 
 
 def _bits(m):
@@ -73,141 +76,157 @@ def rank_program(g, core, T, topo):
     cores = list(T.cores)
     v, sq_, sc = g.vector, g.sync, g.scalar
     S = T.sem
-    ADD, SUB, MAX = AluOpType.add, AluOpType.subtract, AluOpType.max
+    ADD, SUB, MAX, MUL = AluOpType.add, AluOpType.subtract, AluOpType.max, AluOpType.mult
     COPY, SQUARE = ActivationFunctionType.Copy, ActivationFunctionType.Square
     X = AxisListType.X
-    ck = [S.c0, S.c1, S.c2, S.c3]
-    cb = [S.cb0, S.cb1, S.cb2, S.cb3]
-    su = [S.su0, S.su1, S.su2, S.su3]
-    sb = [S.sb0, S.sb1, S.sb2, S.sb3]
-    UP = [T.UP0, T.UP1, T.UP2, T.UP3]
-    PP = [T.PP0, T.PP1, T.PP2, T.PP3]
+    su = [S["su%d" % k] for k in range(NB)]
+    sb = [S["sb%d" % k] for k in range(NB)]
+    sv = [S["sv%d" % k] for k in range(NB)]
+    n9 = [S["n9%d" % k] for k in range(NB)]
+    cb = [S["cb%d" % k] for k in range(NB)]
+    dk = [S["dk%d" % k] for k in range(NB)]
+    yv = [S["yv%d" % k] for k in range(NB)]
+    SP = [T.SP0, T.SP1, T.SP2, T.SP3]
+    DP = [T.DP0, T.DP1, T.DP2, T.DP3]
     left, right = cores[(r - 1) % N], cores[(r + 1) % N]
-    ORDER = (1, 2, 0, 3)
-    PLO = {0: 2, 1: 0, 2: 0, 3: 0}
-    PHI = {0: CW + 3, 1: CW + 3, 2: CW + 3, 3: CW + 1}
-    UHI = {0: CW + 3, 1: CW + 3, 2: CW + 3, 3: CW + 2}
-    OPS = {0: 3, 1: 3, 2: 3, 3: 0}
-    OSB = {0: 0, 1: 0, 2: 0, 3: 3}
-    C_UP, C_P, C_PP, C_Q, C_Y8, C_Y, C_D, C_END = 1, 2, 3, 4, 5, 6, 7, 9
+    SLOT = {1: 0, 2: 1, 3: 2, 0: 3}
+    OFF = {0: 6, 1: 8, 2: 8, 3: 8}
+    NZ = NB + 2
+
+    def fl(t, k):
+        return t[:, CW * SLOT[k]:CW * SLOT[k] + CW]
+
+    def own(k):
+        return T.U4[:, k, OFF[k] + 2:OFF[k] + 2 + CW]
 
     def load_u(q, k):
         lo, hi = max(0, CW * k - 2), min(W, CW * k + CW + 2)
-        q.dma_start(T.U4[:, k, lo - (CW * k - 2):hi - (CW * k - 2)], T.u[:, lo:hi]).then_inc(su[k], 16)
+        q.dma_start(T.U4[:, k, 8:8 + hi - lo], T.u[:, lo:hi]).then_inc(su[k], 16)
 
     def load_b(q, k):
-        q.dma_start(T.B4[:, k, :], T.b[:, CW * k:CW * k + CW]).then_inc(sb[k], 16)
+        q.dma_start(fl(T.BF, k), T.b[:, CW * k:CW * k + CW]).then_inc(sb[k], 16)
 
     sq_.dma_start(T.EB[:, 0:2], T.u[:, 0:2]).then_inc(S.se, 16)
-    sq_.dma_start(T.EB[:, 2:4], T.u[:, W - 2:W]).then_inc(S.se, 16)
+    sc.dma_start(T.EB[:, 2:4], T.u[:, W - 2:W]).then_inc(S.se, 16)
     load_u(sq_, 1)
     load_u(sc, 2)
     load_u(sq_, 0)
+    load_b(sc, 1)
+    load_b(sq_, 2)
+    sc.wait_ge(S.z3, 1)
     load_u(sc, 3)
-    load_b(sq_, 1)
-    load_b(sc, 2)
     load_b(sq_, 0)
     load_b(sc, 3)
 
-    def a_up(k):
+    def a_n9(k):
         sc.wait_ge(su[k], 16)
-        sc.activation(UP[k][:, PLO[k]:UHI[k]], T.U4[:, k, PLO[k]:UHI[k]], COPY).then_inc(ck[k], 1)
-
-    def a_pp(k):
-        sc.wait_ge(ck[k], C_P)
-        sc.activation(PP[k][:, 0:CW], T.P4[:, k, OPS[k]:OPS[k] + CW], COPY).then_inc(ck[k], 1)
+        sc.activation(fl(T.N9, k), own(k), COPY, scale=9.0).then_inc(n9[k], 1)
 
     def a_b(k):
         sc.wait_ge(sb[k], 16)
-        sc.activation(T.B4[:, k, :], T.B4[:, k, :], COPY, scale=4.0).then_inc(cb[k], 1)
-
-    def a_y(k):
-        sc.wait_ge(ck[k], C_Y8)
-        sc.activation(T.Y4[:, k, :], PP[k][:, 0:CW], COPY, scale=0.125).then_inc(ck[k], 1)
+        sc.activation(fl(T.BF, k), fl(T.BF, k), COPY, scale=4.0).then_inc(cb[k], 1)
 
     def a_sq(k):
-        sc.wait_ge(ck[k], C_D)
-        sc.activation(T.SQ4[:, k, :], T.D4[:, k, :], SQUARE, scale=1.0 / math.sqrt(float(N * W)),
-                      accum_out=T.G[:, 8 * r + 2 * k:8 * r + 2 * k + 1]).then_inc(ck[k], 1)
+        sc.wait_ge(sv[k], 3)
+        sc.activation(T.SQ4[:, k, :], T.D4[:, k, :], SQUARE, scale=0.125 / math.sqrt(float(N * W)),
+                      accum_out=T.G[:, 8 * r + 2 * k:8 * r + 2 * k + 1]).then_inc(S.st, 1)
 
-    for k in ORDER:
-        a_up(k)
-    a_pp(1)
-    a_pp(2)
+    def a_dd(k):
+        sc.wait_ge(sv[k], 3)
+        sc.activation(DP[k][:, 0:CW], T.D4[:, k, :], COPY, scale=0.125).then_inc(dk[k], 1)
+
+    a_n9(1)
+    a_n9(2)
     a_b(1)
     a_b(2)
-    a_pp(0)
-    a_pp(3)
+    a_n9(0)
+    a_n9(3)
+    a_sq(1)
+    a_sq(2)
     a_b(0)
     a_b(3)
-    for k in ORDER:
-        a_y(k)
-    for k in ORDER:
-        a_sq(k)
+    a_dd(1)
+    a_dd(2)
+    a_sq(0)
+    a_sq(3)
+    a_dd(0)
+    a_dd(3)
 
-    def v_p(k):
+    v.memset(T.U4[:, 3, XW - 4:XW], 0.0).then_inc(S.z3, 1)
+    for k in range(NB):
+        v.memset(T.U4[:, k, 0:8], 0.0).then_inc(S.z, 1)
+    v.memset(T.CS[:, 0:4 * N - 1], 1.0).then_inc(S.z, 1)
+    v.memset(T.CS[:, 4 * N - 1:4 * N], 0.125).then_inc(S.z, 1)
+    v.wait_ge(S.z, NZ)
+    v.wait_ge(S.z3, 1)
+
+    def v_s(k):
+        o = OFF[k]
         v.wait_ge(su[k], 16)
-        v.wait_ge(ck[k], C_UP)
-        v.tensor_tensor(T.P4[:, k, PLO[k]:PHI[k]], UP[k][:, PLO[k]:PHI[k]], T.U4[:, k, PLO[k] + 1:PHI[k] + 1],
-                        ADD).then_inc(ck[k], 1)
+        v.tensor_tensor_scan(SP[k][:, 0:CW + 4], T.U4[:, k, o:o + CW + 4], T.U4[:, k, o - 5:o + CW - 1], 0.0,
+                             ADD, SUB).then_inc(sv[k], 1)
 
-    def v_q(k):
-        v.wait_ge(ck[k], C_PP)
-        v.tensor_tensor(PP[k][:, 0:CW], PP[k][:, 0:CW], T.P4[:, k, OSB[k]:OSB[k] + CW], ADD).then_inc(ck[k], 1)
-
-    def v_y8(k):
-        v.wait_ge(cb[k], 1)
-        v.wait_ge(ck[k], C_Q)
-        v.tensor_tensor(PP[k][:, 0:CW], PP[k][:, 0:CW], T.B4[:, k, :], ADD).then_inc(ck[k], 1)
+    def v_t(k):
+        v.wait_ge(n9[k], 1)
+        v.wait_ge(sv[k], 1)
+        v.tensor_tensor(SP[k][:, 4:4 + CW], SP[k][:, 4:4 + CW], fl(T.N9, k), SUB).then_inc(sv[k], 1)
 
     def v_d(k):
-        v.wait_ge(ck[k], C_Y)
-        v.tensor_tensor(T.D4[:, k, :], T.Y4[:, k, :], UP[k][:, 2:2 + CW], SUB).then_inc(ck[k], 1)
+        v.wait_ge(cb[k], 1)
+        v.wait_ge(sv[k], 2)
+        v.tensor_tensor(T.D4[:, k, :], SP[k][:, 4:4 + CW], fl(T.BF, k), ADD).then_inc(sv[k], 1)
 
     def v_m(k):
-        v.wait_ge(ck[k], C_D)
+        v.wait_ge(sv[k], 3)
         v.tensor_reduce(T.G[:, 8 * r + 2 * k + 1:8 * r + 2 * k + 2], T.D4[:, k, :], X, MAX,
-                        apply_absolute_value=True).then_inc(ck[k], 1)
+                        apply_absolute_value=True).then_inc(S.st, 1)
+
+    def v_y(k):
+        v.wait_ge(dk[k], 1)
+        v.tensor_tensor(T.Y4[:, k, :], DP[k][:, 0:CW], own(k), ADD).then_inc(yv[k], 1)
 
     hal_n = (len(_bits(_halo_masks(topo, cores, left, cores[(r - 2) % N], core)[1]))
              + len(_bits(_halo_masks(topo, cores, right, core, cores[(r + 2) % N])[0])))
-    for k in ORDER:
-        v_p(k)
-    v_q(1)
-    v_q(2)
-    v_y8(1)
-    v.wait_ge(S.hal, hal_n)
-    v.tensor_tensor(T.P4[:, 0, 0:2], T.U4[:, 0, 0:2], T.U4[:, 0, 1:3], ADD).then_inc(S.vh, 1)
-    v.tensor_tensor(T.P4[:, 3, CW + 1:CW + 3], T.U4[:, 3, CW + 1:CW + 3], T.U4[:, 3, CW + 2:CW + 4], ADD).then_inc(S.vh, 1)
-    v_y8(2)
-    v.wait_ge(S.vh, 2)
-    v_q(0)
-    v_q(3)
-    v_y8(0)
-    v_y8(3)
+    v_s(1)
+    v_s(2)
+    v_s(0)
+    v_t(1)
+    v_t(2)
     v_d(1)
     v_d(2)
     v_m(1)
+    v.wait_ge(S.hal, hal_n)
+    v.tensor_tensor(T.H[:, 1:3], T.H[:, 1:3], T.H[:, 0:4:3], ADD).then_inc(S.vh, 1)
     v_m(2)
+    e0 = CW * SLOT[0] - 2
+    v.wait_ge(S.vh, 1)
+    v.wait_ge(n9[0], 1)
+    v.wait_ge(n9[3], 1)
+    v.tensor_tensor(T.N9[:, e0:e0 + 4], T.N9[:, e0:e0 + 4], T.H[:, 0:4], SUB).then_inc(S.vh, 1)
+    v_s(3)
+    v.wait_ge(S.vh, 2)
+    v_t(0)
+    v_t(3)
     v_d(0)
     v_d(3)
     v_m(0)
     v_m(3)
+    for k in (1, 2, 0, 3):
+        v_y(k)
     g_n = 0
     for d in cores:
         if d != core:
             g_n += len(_bits(_stat_mask(topo, cores, d, core)))
     v.wait_ge(S.gs, g_n)
-    for k in range(NB):
-        v.wait_ge(ck[k], C_END)
-    v.tensor_reduce(T.SO[:, 0:1], T.G[:, 0:8 * N:2], X, ADD).then_inc(S.vf, 1)
-    v.tensor_reduce(T.SO[:, 1:2], T.G[:, 1:8 * N:2], X, MAX).then_inc(S.vf, 1)
+    v.wait_ge(S.st, 2 * NB)
+    v.tensor_reduce(T.R[:, 8 * N - 2:8 * N - 1], T.G[:, 0:8 * N:2], X, ADD).then_inc(S.vf, 1)
+    v.tensor_tensor_scan(T.R[:, 1:8 * N:2], T.G[:, 1:8 * N:2], T.CS[:, 0:4 * N], 0.0, MAX, MUL).then_inc(S.vf, 1)
 
-    for k in ORDER:
-        sq_.wait_ge(ck[k], C_Y)
+    for k in (1, 2, 0, 3):
+        sq_.wait_ge(yv[k], 1)
         sq_.dma_start(T.y[:, CW * k:CW * k + CW], T.Y4[:, k, :]).then_inc(S.sy, 16)
     sq_.wait_ge(S.vf, 2)
-    sq_.dma_start(T.s[:], T.SO[:]).then_inc(S.ss, 16)
+    sq_.dma_start(T.s[:], T.R[:, 8 * N - 2:8 * N]).then_inc(S.ss, 16)
     sq_.wait_ge(S.sy, 64)
     sq_.wait_ge(S.ss, 16)
 
@@ -218,12 +237,11 @@ def rank_program(g, core, T, topo):
     ml, mr = _halo_masks(topo, cores, core, left, right)
     g.wait_ge(S.se, 32)
     g.remote_dma_fused([
-        RemoteDMATransfer(dst_ids=[dst(left)], dma_engine_mask=ml, remote_sem=S.hal, src=T.EB[:, 0:2],
-                          dst=T.U4[:, NB - 1, CW + 2:CW + 4]),
-        RemoteDMATransfer(dst_ids=[dst(right)], dma_engine_mask=mr, remote_sem=S.hal, src=T.EB[:, 2:4], dst=T.U4[:, 0, 0:2]),
+        RemoteDMATransfer(dst_ids=[dst(left)], dma_engine_mask=ml, remote_sem=S.hal, src=T.EB[:, 0:2], dst=T.H[:, 0:2]),
+        RemoteDMATransfer(dst_ids=[dst(right)], dma_engine_mask=mr, remote_sem=S.hal, src=T.EB[:, 2:4], dst=T.H[:, 2:4]),
     ], local_sem=S.loc)
     loc_n = len(_bits(ml)) + len(_bits(mr))
-    own = T.G[:, 8 * r:8 * r + 8]
+    mine = T.G[:, 8 * r:8 * r + 8]
     groups = {}
     for d in cores:
         if d != core:
@@ -232,9 +250,8 @@ def rank_program(g, core, T, topo):
     for m in sorted(groups):
         ds = groups[m]
         trs.append(RemoteDMATransfer(dst_ids=[dst(d) for d in ds], dma_engine_mask=m, remote_sem=S.gs,
-                                     srcs=[own], dsts=[own for d in ds]))
+                                     srcs=[mine], dsts=[mine for d in ds]))
         loc_n += len(_bits(m))
-    for k in range(NB):
-        g.wait_ge(ck[k], C_END)
+    g.wait_ge(S.st, 2 * NB)
     g.remote_dma_fused(trs, local_sem=S.loc)
     g.wait_ge(S.loc, loc_n)

@@ -7,6 +7,7 @@ W = 1024
 CW = 256
 NB = 4
 XW = CW + 12
+TB = 2
 
 SCRATCH = {
     "U4": ("sbuf", [128, NB, XW], "float32"),
@@ -20,16 +21,21 @@ SCRATCH = {
     "G": ("sbuf", [128, 8 * N], "float32"),
     "CS": ("sbuf", [128, 4 * N], "float32"),
     "R": ("sbuf", [128, 8 * N], "float32"),
+    "ON": ("sbuf", [128, 128], "float32"),
+    "I1": ("sbuf", [128, 128], "float32"),
+    "IM9": ("sbuf", [128, 128], "float32"),
+    "I4": ("sbuf", [128, 128], "float32"),
+    "SB": ("sbuf", [128, CW + 4], "float32"),
     "SP0": ("psum", [128, 512], "float32"),
     "SP1": ("psum", [128, 512], "float32"),
-    "SP2": ("psum", [128, 512], "float32"),
+    "ZP": ("psum", [128, 512], "float32"),
     "SP3": ("psum", [128, 512], "float32"),
     "DP0": ("psum", [128, 512], "float32"),
     "DP1": ("psum", [128, 512], "float32"),
     "DP2": ("psum", [128, 512], "float32"),
     "DP3": ("psum", [128, 512], "float32"),
 }
-SEMAPHORES = (["z", "z3", "se", "st", "vh", "hal", "gs", "loc", "sy", "vf", "ss"]
+SEMAPHORES = (["z", "z3", "zo", "zi", "zm", "zt", "q2", "se", "st", "vh", "hal", "gs", "loc", "sy", "vf", "ss"]
               + [p + "%d" % k for p in ("su", "sb", "sv", "n9", "cb", "dk", "yv") for k in range(NB)])
 
 
@@ -74,7 +80,7 @@ def rank_program(g, core, T, topo):
     if r is None:
         return
     cores = list(T.cores)
-    v, sq_, sc = g.vector, g.sync, g.scalar
+    v, sq_, sc, te = g.vector, g.sync, g.scalar, g.tensor
     S = T.sem
     ADD, SUB, MAX, MUL = AluOpType.add, AluOpType.subtract, AluOpType.max, AluOpType.mult
     COPY, SQUARE = ActivationFunctionType.Copy, ActivationFunctionType.Square
@@ -86,15 +92,16 @@ def rank_program(g, core, T, topo):
     cb = [S["cb%d" % k] for k in range(NB)]
     dk = [S["dk%d" % k] for k in range(NB)]
     yv = [S["yv%d" % k] for k in range(NB)]
-    SP = [T.SP0, T.SP1, T.SP2, T.SP3]
+    SP = [T.SP0, T.SP1, None, T.SP3]
     DP = [T.DP0, T.DP1, T.DP2, T.DP3]
     left, right = cores[(r - 1) % N], cores[(r + 1) % N]
-    SLOT = {1: 0, 2: 1, 3: 2, 0: 3}
     OFF = {0: 6, 1: 8, 2: 8, 3: 8}
     NZ = NB + 2
+    SQS = 0.125 / math.sqrt(float(N * W))
+    DONE = {0: 4, 1: 3, 3: 4}
 
     def fl(t, k):
-        return t[:, CW * SLOT[k]:CW * SLOT[k] + CW]
+        return t[:, CW * k:CW * k + CW]
 
     def own(k):
         return T.U4[:, k, OFF[k] + 2:OFF[k] + 2 + CW]
@@ -108,13 +115,13 @@ def rank_program(g, core, T, topo):
 
     sq_.dma_start(T.EB[:, 0:2], T.u[:, 0:2]).then_inc(S.se, 16)
     sc.dma_start(T.EB[:, 2:4], T.u[:, W - 2:W]).then_inc(S.se, 16)
-    load_u(sq_, 1)
-    load_u(sc, 2)
+    load_u(sq_, 2)
+    load_u(sc, 1)
     load_u(sq_, 0)
     load_b(sc, 1)
-    load_b(sq_, 2)
-    sc.wait_ge(S.z3, 1)
-    load_u(sc, 3)
+    sq_.wait_ge(S.z3, 1)
+    load_u(sq_, 3)
+    load_b(sc, 2)
     load_b(sq_, 0)
     load_b(sc, 3)
 
@@ -127,31 +134,45 @@ def rank_program(g, core, T, topo):
         sc.activation(fl(T.BF, k), fl(T.BF, k), COPY, scale=4.0).then_inc(cb[k], 1)
 
     def a_sq(k):
-        sc.wait_ge(sv[k], 3)
-        sc.activation(T.SQ4[:, k, :], T.D4[:, k, :], SQUARE, scale=0.125 / math.sqrt(float(N * W)),
+        sc.wait_ge(sv[k], DONE[k])
+        sc.activation(T.SQ4[:, k, :], T.D4[:, k, :], SQUARE, scale=SQS,
                       accum_out=T.G[:, 8 * r + 2 * k:8 * r + 2 * k + 1]).then_inc(S.st, 1)
 
     def a_dd(k):
-        sc.wait_ge(sv[k], 3)
+        sc.wait_ge(sv[k], DONE[k])
         sc.activation(DP[k][:, 0:CW], T.D4[:, k, :], COPY, scale=0.125).then_inc(dk[k], 1)
 
+    sc.wait_ge(S.zi, 1)
+    sc.activation(T.IM9[:, :], T.I1[:, :], COPY, scale=-9.0).then_inc(S.zm, 1)
+    sc.activation(T.I4[:, :], T.I1[:, :], COPY, scale=4.0).then_inc(S.zm, 1)
     a_n9(1)
-    a_n9(2)
-    a_b(1)
-    a_b(2)
     a_n9(0)
+    a_b(1)
     a_n9(3)
     a_sq(1)
-    a_sq(2)
     a_b(0)
     a_b(3)
-    a_dd(1)
-    a_dd(2)
+    sc.wait_ge(S.zt, 1)
+    sc.activation(T.SQ4[:, TB, :], T.ZP[:, 0:CW], SQUARE, scale=SQS,
+                  accum_out=T.G[:, 8 * r + 2 * TB:8 * r + 2 * TB + 1]).then_inc(S.q2, 1)
     a_sq(0)
     a_sq(3)
+    a_dd(1)
+    sc.wait_ge(S.q2, 2)
+    sc.activation(DP[TB][:, 0:CW], T.ZP[:, 0:CW], COPY, scale=0.125).then_inc(dk[TB], 1)
     a_dd(0)
     a_dd(3)
 
+    te.wait_ge(S.zm, 2)
+    te.wait_ge(su[TB], 16)
+    te.matmul(T.ZP[:, 0:CW], T.IM9[:, :], own(TB), True, False)
+    te.wait_ge(S.zi, 1)
+    te.wait_ge(sv[TB], 1)
+    te.matmul(T.ZP[:, 0:CW], T.I1[:, :], T.SB[:, 4:4 + CW], False, False)
+    te.wait_ge(sb[TB], 16)
+    te.matmul(T.ZP[:, 0:CW], T.I4[:, :], fl(T.BF, TB), False, True).then_inc(S.zt, 1)
+
+    v.memset(T.ON[:, :], 1.0).then_inc(S.zo, 1)
     v.memset(T.U4[:, 3, XW - 4:XW], 0.0).then_inc(S.z3, 1)
     for k in range(NB):
         v.memset(T.U4[:, k, 0:8], 0.0).then_inc(S.z, 1)
@@ -162,8 +183,9 @@ def rank_program(g, core, T, topo):
 
     def v_s(k):
         o = OFF[k]
+        out = T.SB[:, 0:CW + 4] if k == TB else SP[k][:, 0:CW + 4]
         v.wait_ge(su[k], 16)
-        v.tensor_tensor_scan(SP[k][:, 0:CW + 4], T.U4[:, k, o:o + CW + 4], T.U4[:, k, o - 5:o + CW - 1], 0.0,
+        v.tensor_tensor_scan(out, T.U4[:, k, o:o + CW + 4], T.U4[:, k, o - 5:o + CW - 1], 0.0,
                              ADD, SUB).then_inc(sv[k], 1)
 
     def v_t(k):
@@ -177,7 +199,7 @@ def rank_program(g, core, T, topo):
         v.tensor_tensor(T.D4[:, k, :], SP[k][:, 4:4 + CW], fl(T.BF, k), ADD).then_inc(sv[k], 1)
 
     def v_m(k):
-        v.wait_ge(sv[k], 3)
+        v.wait_ge(sv[k], DONE[k])
         v.tensor_reduce(T.G[:, 8 * r + 2 * k + 1:8 * r + 2 * k + 2], T.D4[:, k, :], X, MAX,
                         apply_absolute_value=True).then_inc(S.st, 1)
 
@@ -187,28 +209,27 @@ def rank_program(g, core, T, topo):
 
     hal_n = (len(_bits(_halo_masks(topo, cores, left, cores[(r - 2) % N], core)[1]))
              + len(_bits(_halo_masks(topo, cores, right, core, cores[(r + 2) % N])[0])))
-    v_s(1)
     v_s(2)
+    v_s(1)
     v_s(0)
     v_t(1)
-    v_t(2)
     v_d(1)
-    v_d(2)
-    v_m(1)
-    v.wait_ge(S.hal, hal_n)
-    v.tensor_tensor(T.H[:, 1:3], T.H[:, 1:3], T.H[:, 0:4:3], ADD).then_inc(S.vh, 1)
-    v_m(2)
-    e0 = CW * SLOT[0] - 2
-    v.wait_ge(S.vh, 1)
-    v.wait_ge(n9[0], 1)
-    v.wait_ge(n9[3], 1)
-    v.tensor_tensor(T.N9[:, e0:e0 + 4], T.N9[:, e0:e0 + 4], T.H[:, 0:4], SUB).then_inc(S.vh, 1)
     v_s(3)
-    v.wait_ge(S.vh, 2)
+    v_m(1)
     v_t(0)
     v_t(3)
     v_d(0)
+    v.wait_ge(S.hal, hal_n)
+    v.tensor_tensor(T.H[:, 1:3], T.H[:, 1:3], T.H[:, 0:4:3], ADD).then_inc(S.vh, 1)
     v_d(3)
+    v.wait_ge(S.vh, 1)
+    v.wait_ge(sv[0], 3)
+    v.tensor_tensor(T.D4[:, 0, 0:2], T.D4[:, 0, 0:2], T.H[:, 2:4], ADD).then_inc(sv[0], 1)
+    v.wait_ge(S.q2, 1)
+    v.tensor_reduce(T.G[:, 8 * r + 2 * TB + 1:8 * r + 2 * TB + 2], T.ZP[:, 0:CW], X, MAX,
+                    apply_absolute_value=True).then_inc(S.q2, 1)
+    v.wait_ge(sv[3], 3)
+    v.tensor_tensor(T.D4[:, 3, CW - 2:CW], T.D4[:, 3, CW - 2:CW], T.H[:, 0:2], ADD).then_inc(sv[3], 1)
     v_m(0)
     v_m(3)
     for k in (1, 2, 0, 3):
@@ -218,7 +239,8 @@ def rank_program(g, core, T, topo):
         if d != core:
             g_n += len(_bits(_stat_mask(topo, cores, d, core)))
     v.wait_ge(S.gs, g_n)
-    v.wait_ge(S.st, 2 * NB)
+    v.wait_ge(S.st, 2 * NB - 2)
+    v.wait_ge(S.q2, 2)
     v.tensor_reduce(T.R[:, 8 * N - 2:8 * N - 1], T.G[:, 0:8 * N:2], X, ADD).then_inc(S.vf, 1)
     v.tensor_tensor_scan(T.R[:, 1:8 * N:2], T.G[:, 1:8 * N:2], T.CS[:, 0:4 * N], 0.0, MAX, MUL).then_inc(S.vf, 1)
 
@@ -234,6 +256,8 @@ def rank_program(g, core, T, topo):
         rid, pid = topo.addr(d, core)
         return DstId(rid=rid, pnc=pid)
 
+    g.wait_ge(S.zo, 1)
+    g.affine_select(T.I1[:, :], T.ON[:, :], [[-1, 128]], AluOpType.is_equal, 0.0, 0, 1).then_inc(S.zi, 1)
     ml, mr = _halo_masks(topo, cores, core, left, right)
     g.wait_ge(S.se, 32)
     g.remote_dma_fused([
@@ -252,6 +276,7 @@ def rank_program(g, core, T, topo):
         trs.append(RemoteDMATransfer(dst_ids=[dst(d) for d in ds], dma_engine_mask=m, remote_sem=S.gs,
                                      srcs=[mine], dsts=[mine for d in ds]))
         loc_n += len(_bits(m))
-    g.wait_ge(S.st, 2 * NB)
+    g.wait_ge(S.st, 2 * NB - 2)
+    g.wait_ge(S.q2, 2)
     g.remote_dma_fused(trs, local_sem=S.loc)
     g.wait_ge(S.loc, loc_n)

import math
from concourse.bass import DstId, RemoteDMATransfer
from concourse.mybir import AluOpType, AxisListType, ActivationFunctionType

N = 6
W = 1024
CW = 256
NB = 4
XW = CW + 12
TB = 2

SCRATCH = {
    "U4": ("sbuf", [128, NB, XW], "float32"),
    "BF": ("sbuf", [128, W], "float32"),
    "N9": ("sbuf", [128, W], "float32"),
    "EB": ("sbuf", [128, 4], "float32"),
    "H": ("sbuf", [128, 4], "float32"),
    "D4": ("sbuf", [128, NB, CW], "float32"),
    "SQ4": ("sbuf", [128, NB, CW], "float32"),
    "Y4": ("sbuf", [128, NB, CW], "float32"),
    "G": ("sbuf", [128, 8 * N], "float32"),
    "CS": ("sbuf", [128, 4 * N], "float32"),
    "R": ("sbuf", [128, 8 * N], "float32"),
    "ON": ("sbuf", [128, 128], "float32"),
    "I1": ("sbuf", [128, 128], "float32"),
    "IM9": ("sbuf", [128, 128], "float32"),
    "I4": ("sbuf", [128, 128], "float32"),
    "SB": ("sbuf", [128, CW + 4], "float32"),
    "SP0": ("psum", [128, 512], "float32"),
    "SP1": ("psum", [128, 512], "float32"),
    "ZP": ("psum", [128, 512], "float32"),
    "SP3": ("psum", [128, 512], "float32"),
    "DP0": ("psum", [128, 512], "float32"),
    "DP1": ("psum", [128, 512], "float32"),
    "DP2": ("psum", [128, 512], "float32"),
    "DP3": ("psum", [128, 512], "float32"),
}
SEMAPHORES = (["z", "z3", "zo", "zi", "zm", "zt", "q2", "se", "st", "vh", "hal", "gs", "loc", "sy", "vf", "ss"]
              + [p + "%d" % k for p in ("su", "sb", "sv", "n9", "cb", "dk", "yv") for k in range(NB)])


def _bits(m):
    return [i for i in range(m.bit_length()) if (m >> i) & 1]


def _mk(bits):
    m = 0
    for i in bits:
        m |= 1 << i
    return m


def _low(topo, cores, c):
    low = -1
    for d in cores:
        if d != c:
            low &= topo.mask(c, d)
    return low


def _halo_masks(topo, cores, c, dl, dr):
    low = _low(topo, cores, c)
    hl, hr = topo.mask(c, dl) & ~low, topo.mask(c, dr) & ~low
    if hr:
        return low, hr
    if hl:
        return hl, low
    b = _bits(low)
    return _mk(b[:len(b) // 2]), _mk(b[len(b) // 2:])


def _stat_mask(topo, cores, c, d):
    low = _low(topo, cores, c)
    hi = topo.mask(c, d) & ~low
    return hi if hi else low


def rank_program(g, core, T, topo):
    r = T.rank_of(core)
    if r is None:
        return
    cores = list(T.cores)
    v, sq_, sc, te = g.vector, g.sync, g.scalar, g.tensor
    S = T.sem
    ADD, SUB, MAX, MUL = AluOpType.add, AluOpType.subtract, AluOpType.max, AluOpType.mult
    COPY, SQUARE = ActivationFunctionType.Copy, ActivationFunctionType.Square
    X = AxisListType.X
    su = [S["su%d" % k] for k in range(NB)]
    sb = [S["sb%d" % k] for k in range(NB)]
    sv = [S["sv%d" % k] for k in range(NB)]
    n9 = [S["n9%d" % k] for k in range(NB)]
    cb = [S["cb%d" % k] for k in range(NB)]
    dk = [S["dk%d" % k] for k in range(NB)]
    yv = [S["yv%d" % k] for k in range(NB)]
    SP = [T.SP0, T.SP1, None, T.SP3]
    DP = [T.DP0, T.DP1, T.DP2, T.DP3]
    left, right = cores[(r - 1) % N], cores[(r + 1) % N]
    OFF = {0: 6, 1: 8, 2: 8, 3: 8}
    NZ = NB + 2
    SQS = 0.125 / math.sqrt(float(N * W))
    DONE = {0: 4, 1: 3, 3: 4}

    def fl(t, k):
        return t[:, CW * k:CW * k + CW]

    def own(k):
        return T.U4[:, k, OFF[k] + 2:OFF[k] + 2 + CW]

    def load_u(q, k):
        lo, hi = max(0, CW * k - 2), min(W, CW * k + CW + 2)
        q.dma_start(T.U4[:, k, 8:8 + hi - lo], T.u[:, lo:hi]).then_inc(su[k], 16)

    def load_b(q, k):
        q.dma_start(fl(T.BF, k), T.b[:, CW * k:CW * k + CW]).then_inc(sb[k], 16)

    sq_.dma_start(T.EB[:, 0:2], T.u[:, 0:2]).then_inc(S.se, 16)
    sc.dma_start(T.EB[:, 2:4], T.u[:, W - 2:W]).then_inc(S.se, 16)
    load_u(sq_, 2)
    load_u(sc, 1)
    load_u(sq_, 0)
    load_b(sc, 1)
    sq_.wait_ge(S.z3, 1)
    load_u(sq_, 3)
    load_b(sc, 2)
    load_b(sq_, 0)
    load_b(sc, 3)

    def a_n9(k):
        sc.wait_ge(su[k], 16)
        sc.activation(fl(T.N9, k), own(k), COPY, scale=9.0).then_inc(n9[k], 1)

    def a_b(k):
        sc.wait_ge(sb[k], 16)
        sc.activation(fl(T.BF, k), fl(T.BF, k), COPY, scale=4.0).then_inc(cb[k], 1)

    def a_sq(k):
        sc.wait_ge(sv[k], DONE[k])
        sc.activation(T.SQ4[:, k, :], T.D4[:, k, :], SQUARE, scale=SQS,
                      accum_out=T.G[:, 8 * r + 2 * k:8 * r + 2 * k + 1]).then_inc(S.st, 1)

    def a_dd(k):
        sc.wait_ge(sv[k], DONE[k])
        sc.activation(DP[k][:, 0:CW], T.D4[:, k, :], COPY, scale=0.125).then_inc(dk[k], 1)

    sc.wait_ge(S.zi, 1)
    sc.activation(T.IM9[:, :], T.I1[:, :], COPY, scale=-9.0).then_inc(S.zm, 1)
    sc.activation(T.I4[:, :], T.I1[:, :], COPY, scale=4.0).then_inc(S.zm, 1)
    a_n9(1)
    a_n9(0)
    a_b(1)
    a_n9(3)
    a_sq(1)
    a_b(0)
    a_b(3)
    sc.wait_ge(S.zt, 1)
    sc.activation(T.SQ4[:, TB, :], T.ZP[:, 0:CW], SQUARE, scale=SQS,
                  accum_out=T.G[:, 8 * r + 2 * TB:8 * r + 2 * TB + 1]).then_inc(S.q2, 1)
    a_sq(0)
    a_sq(3)
    a_dd(1)
    sc.wait_ge(S.q2, 2)
    sc.activation(DP[TB][:, 0:CW], T.ZP[:, 0:CW], COPY, scale=0.125).then_inc(dk[TB], 1)
    a_dd(0)
    a_dd(3)

    te.wait_ge(S.zm, 2)
    te.wait_ge(su[TB], 16)
    te.matmul(T.ZP[:, 0:CW], T.IM9[:, :], own(TB), True, False)
    te.wait_ge(S.zi, 1)
    te.wait_ge(sv[TB], 1)
    te.matmul(T.ZP[:, 0:CW], T.I1[:, :], T.SB[:, 4:4 + CW], False, False)
    te.wait_ge(sb[TB], 16)
    te.matmul(T.ZP[:, 0:CW], T.I4[:, :], fl(T.BF, TB), False, True).then_inc(S.zt, 1)

    v.memset(T.ON[:, :], 1.0).then_inc(S.zo, 1)
    v.memset(T.U4[:, 3, XW - 4:XW], 0.0).then_inc(S.z3, 1)
    for k in range(NB):
        v.memset(T.U4[:, k, 0:8], 0.0).then_inc(S.z, 1)
    v.memset(T.CS[:, 0:4 * N - 1], 1.0).then_inc(S.z, 1)
    v.memset(T.CS[:, 4 * N - 1:4 * N], 0.125).then_inc(S.z, 1)
    v.wait_ge(S.z, NZ)
    v.wait_ge(S.z3, 1)

    def v_s(k):
        o = OFF[k]
        out = T.SB[:, 0:CW + 4] if k == TB else SP[k][:, 0:CW + 4]
        v.wait_ge(su[k], 16)
        v.tensor_tensor_scan(out, T.U4[:, k, o:o + CW + 4], T.U4[:, k, o - 5:o + CW - 1], 0.0,
                             ADD, SUB).then_inc(sv[k], 1)

    def v_t(k):
        v.wait_ge(n9[k], 1)
        v.wait_ge(sv[k], 1)
        v.tensor_tensor(SP[k][:, 4:4 + CW], SP[k][:, 4:4 + CW], fl(T.N9, k), SUB).then_inc(sv[k], 1)

    def v_d(k):
        v.wait_ge(cb[k], 1)
        v.wait_ge(sv[k], 2)
        v.tensor_tensor(T.D4[:, k, :], SP[k][:, 4:4 + CW], fl(T.BF, k), ADD).then_inc(sv[k], 1)

    def v_m(k):
        v.wait_ge(sv[k], DONE[k])
        v.tensor_reduce(T.G[:, 8 * r + 2 * k + 1:8 * r + 2 * k + 2], T.D4[:, k, :], X, MAX,
                        apply_absolute_value=True).then_inc(S.st, 1)

    def v_y(k):
        v.wait_ge(dk[k], 1)
        v.tensor_tensor(T.Y4[:, k, :], DP[k][:, 0:CW], own(k), ADD).then_inc(yv[k], 1)

    hal_n = (len(_bits(_halo_masks(topo, cores, left, cores[(r - 2) % N], core)[1]))
             + len(_bits(_halo_masks(topo, cores, right, core, cores[(r + 2) % N])[0])))
    v_s(2)
    v_s(1)
    v_s(0)
    v_t(1)
    v_d(1)
    v_s(3)
    v_m(1)
    v_t(0)
    v_t(3)
    v_d(0)
    v.wait_ge(S.hal, hal_n)
    v.tensor_tensor(T.H[:, 1:3], T.H[:, 1:3], T.H[:, 0:4:3], ADD).then_inc(S.vh, 1)
    v_d(3)
    v.wait_ge(S.vh, 1)
    v.wait_ge(sv[0], 3)
    v.tensor_tensor(T.D4[:, 0, 0:2], T.D4[:, 0, 0:2], T.H[:, 2:4], ADD).then_inc(sv[0], 1)
    v.wait_ge(S.q2, 1)
    v.tensor_reduce(T.G[:, 8 * r + 2 * TB + 1:8 * r + 2 * TB + 2], T.ZP[:, 0:CW], X, MAX,
                    apply_absolute_value=True).then_inc(S.q2, 1)
    v.wait_ge(sv[3], 3)
    v.tensor_tensor(T.D4[:, 3, CW - 2:CW], T.D4[:, 3, CW - 2:CW], T.H[:, 0:2], ADD).then_inc(sv[3], 1)
    v_m(0)
    v_m(3)
    for k in (1, 2, 0, 3):
        v_y(k)
    g_n = 0
    for d in cores:
        if d != core:
            g_n += len(_bits(_stat_mask(topo, cores, d, core)))
    v.wait_ge(S.gs, g_n)
    v.wait_ge(S.st, 2 * NB - 2)
    v.wait_ge(S.q2, 2)
    v.tensor_reduce(T.R[:, 8 * N - 2:8 * N - 1], T.G[:, 0:8 * N:2], X, ADD).then_inc(S.vf, 1)
    v.tensor_tensor_scan(T.R[:, 1:8 * N:2], T.G[:, 1:8 * N:2], T.CS[:, 0:4 * N], 0.0, MAX, MUL).then_inc(S.vf, 1)

    for k in (1, 2, 0, 3):
        sq_.wait_ge(yv[k], 1)
        sq_.dma_start(T.y[:, CW * k:CW * k + CW], T.Y4[:, k, :]).then_inc(S.sy, 16)
    sq_.wait_ge(S.vf, 2)
    sq_.dma_start(T.s[:], T.R[:, 8 * N - 2:8 * N]).then_inc(S.ss, 16)
    sq_.wait_ge(S.sy, 64)
    sq_.wait_ge(S.ss, 16)

    def dst(d):
        rid, pid = topo.addr(d, core)
        return DstId(rid=rid, pnc=pid)

    g.wait_ge(S.zo, 1)
    g.affine_select(T.I1[:, :], T.ON[:, :], [[-1, 128]], AluOpType.is_equal, 0.0, 0, 1).then_inc(S.zi, 1)
    ml, mr = _halo_masks(topo, cores, core, left, right)
    g.wait_ge(S.se, 32)
    g.remote_dma_fused([
        RemoteDMATransfer(dst_ids=[dst(left)], dma_engine_mask=ml, remote_sem=S.hal, src=T.EB[:, 0:2], dst=T.H[:, 0:2]),
        RemoteDMATransfer(dst_ids=[dst(right)], dma_engine_mask=mr, remote_sem=S.hal, src=T.EB[:, 2:4], dst=T.H[:, 2:4]),
    ], local_sem=S.loc)
    loc_n = len(_bits(ml)) + len(_bits(mr))
    mine = T.G[:, 8 * r:8 * r + 8]
    groups = {}
    for d in cores:
        if d != core:
            groups.setdefault(_stat_mask(topo, cores, core, d), []).append(d)
    trs = []
    for m in sorted(groups):
        ds = groups[m]
        trs.append(RemoteDMATransfer(dst_ids=[dst(d) for d in ds], dma_engine_mask=m, remote_sem=S.gs,
                                     srcs=[mine], dsts=[mine for d in ds]))
        loc_n += len(_bits(m))
    g.wait_ge(S.st, 2 * NB - 2)
    g.wait_ge(S.q2, 2)
    g.remote_dma_fused(trs, local_sem=S.loc)
    g.wait_ge(S.loc, loc_n)
